import numpy as np
import ml_dtypes


def mxq(x, axis, fmt="e4m3"):
    dtype, down = {"e4m3": (ml_dtypes.float8_e4m3fn, 7), "e5m2": (ml_dtypes.float8_e5m2, 14)}[fmt]
    v = np.moveaxis(np.asarray(x, np.float32).astype(ml_dtypes.bfloat16).astype(np.float64), axis, -1)
    blocks = v.reshape(v.shape[:-1] + (-1, 32))
    amax = np.abs(blocks).max(-1, keepdims=True)
    byte = np.maximum(np.where(amax > 0, np.frexp(amax)[1] - 1 + 127, 0) - down, 1)
    scale = np.exp2(byte - 127.0)
    codes = (blocks / scale).astype(np.float32).astype(dtype).astype(np.float64)
    return np.moveaxis((codes * scale).reshape(v.shape), -1, axis)


WIDE = False


def mx_kscale(k):
    if not WIDE:
        return np.ones(k)
    levels = np.array([10, -10, 5, -5, 0])
    if k % 512:
        return np.exp2(np.random.permutation(np.resize(levels, k // 32))).repeat(32)
    a = np.empty((k // 512, 16))
    for p in range(k // 512):
        a[p, :8] = np.random.permutation(np.resize(levels, 8))
        for g in range(8):
            far = levels[np.abs(levels - a[p, g]) >= 10]
            a[p, g + 8] = far[np.random.randint(len(far))]
    return np.exp2(a.ravel()).repeat(32)


def f64(x):
    return np.asarray(x).astype(np.float64)


def striped(idx):
    return np.tile(idx.reshape(-1, 16).T, (8, 1)).astype(np.uint16)


def unstriped(offs):
    return offs[:16].T.reshape(-1).astype(np.int64)


def pack_weight(w):
    k, n = w.shape
    w = f64(np.asarray(w, np.float32).astype(ml_dtypes.bfloat16)).reshape(k // 32, 32, n)
    amax = np.abs(w).max(1)
    byte = np.clip(np.where(amax > 0, np.frexp(amax)[1] - 1 + 127 - 7, 1), 1, 254)
    scaled = (w * np.exp2(127.0 - byte)[:, None, :]).reshape(k, n).astype(np.float32)
    words = np.ascontiguousarray(scaled.reshape(k // 512, 128, 4, n).transpose(0, 1, 3, 2)).astype(ml_dtypes.float8_e4m3fn).view(np.uint8)
    return words, np.ascontiguousarray(byte.astype(np.uint8).reshape(k // 512, 16, n))


def unpack_weight(words, scales):
    g, p, n, _ = words.shape
    vals = np.ascontiguousarray(words).view(ml_dtypes.float8_e4m3fn).astype(np.float64) * np.repeat(np.exp2(scales.astype(np.float64) - 127.0), 8, axis=1)[..., None]
    return vals.transpose(0, 1, 3, 2).reshape(g * 512, n)


E2M1 = np.array([0.0, 0.5, 1.0, 1.5, 2.0, 3.0, 4.0, 6.0, -0.0, -0.5, -1.0, -1.5, -2.0, -3.0, -4.0, -6.0])


def pack_fp4(w):
    k, n = w.shape
    w = f64(np.asarray(w, np.float32).astype(ml_dtypes.bfloat16)).reshape(k // 32, 32, n)
    amax = np.abs(w).max(1)
    mant, ex = np.frexp(amax / 6.0)
    byte = np.clip(np.where(amax > 0, np.where(mant > 0.5, ex, ex - 1) + 127, 1), 1, 254)
    scaled = (w * np.exp2(127.0 - byte)[:, None, :]).reshape(k, n).astype(np.float32)
    c = np.ascontiguousarray(scaled.reshape(k // 512, 128, 4, n).transpose(0, 1, 3, 2)).astype(ml_dtypes.float4_e2m1fn).view(np.uint8) & 0xF
    words = (c[..., 0::2] | (c[..., 1::2] << 4)).reshape(k // 512, 128, 2 * n)
    return np.ascontiguousarray(words), np.ascontiguousarray(byte.astype(np.uint8).reshape(k // 512, 16, n))


def unpack_fp4(words, scales):
    g, _, n = scales.shape
    words = np.ascontiguousarray(words).reshape(g, 128, n, 2)
    nib = np.empty((g, 128, n, 4), np.uint8)
    nib[..., 0::2] = words & 0xF
    nib[..., 1::2] = words >> 4
    vals = E2M1[nib] * np.repeat(np.exp2(scales.astype(np.float64) - 127.0), 8, axis=1)[..., None]
    return vals.transpose(0, 1, 3, 2).reshape(g * 512, n)


def gelu(v):
    return 0.5 * v * (1.0 + np.tanh(np.sqrt(2.0 / np.pi) * (v + 0.044715 * v**3)))


K, T, S, V, H, N, J = 1024, 2048, 1024, 512, 512, 128, 512


def setup_inputs():
    n = np.random.standard_normal
    s = mx_kscale(K)[:, None]
    u = mx_kscale(H)
    r = mx_kscale(J)[:, None]
    packed_xT = pack_weight(n((K, T)) * s)
    packed_w4 = pack_fp4(n((H, N)) / np.sqrt(H) / u[:, None])
    return {
        "x_words": packed_xT[0],
        "x_scales": packed_xT[1],
        "eT": (n((J, V)) * r).astype(np.float32),
        "w1": (n((K, H)) / np.sqrt(3 * K) / s * u).astype(np.float32),
        "w2": (n((K, H)) / np.sqrt(3 * K) / s * u).astype(np.float32),
        "w3": (n((J, H)) / np.sqrt(3 * J) / r * u).astype(np.float32),
        "w4_words": packed_w4[0],
        "w4_scales": packed_w4[1],
        "offs": striped(np.random.permutation(T)[:S]),
    }


def reference(x_words, x_scales, eT, w1, w2, w3, w4_words, w4_scales, offs):
    xq = unpack_weight(x_words, x_scales)[:, unstriped(offs)]
    h = gelu(mxq(f64(w1), 0, "e4m3").T @ xq[:, :V] + mxq(f64(w2), 0, "e4m3").T @ xq[:, V:2 * V] + mxq(f64(w3), 0, "e4m3").T @ mxq(f64(eT), 0, "e4m3"))
    return unpack_fp4(w4_words, w4_scales).T @ mxq(h, 0, "e4m3")

@@ -1,0 +1,174 @@
+from contextlib import ExitStack
+
+import concourse.mybir as mybir
+from concourse.masks import make_identity
+
+K, T, S, V, H, N, J = 1024, 2048, 1024, 512, 512, 128, 512
+FLOPS = 2 * (2 * K * H * V + J * H * V + H * N * V)
+
+F32 = mybir.dt.float32
+BF16 = mybir.dt.bfloat16
+I32 = mybir.dt.int32
+U32 = mybir.dt.uint32
+U16 = mybir.dt.uint16
+U8 = mybir.dt.uint8
+FP8X4 = mybir.dt.float8_e4m3fn_x4
+FP4X4 = mybir.dt.float4_e2m1fn_x4
+GELU = mybir.ActivationFunctionType.Gelu_apprx_tanh
+
+P = 128
+PACK = 4
+K_PASS = P * PACK
+EDGES = 128
+CHUNKS = V // EDGES
+E_LOADS = ((0, 256), (256, 384), (384, 512))
+VECTOR_SHARE = 336
+
+
+def tile_picked_edgeup_gelu_p_kernel(
+    tc, x_words, x_scales, eT, w1, w2, w3, w4_words, w4_scales, offs, out
+):
+    nc = tc.nc
+    with ExitStack() as ctx:
+        keep = ctx.enter_context(tc.tile_pool(name="keep", bufs=1))
+        ring = ctx.enter_context(tc.tile_pool(name="ring", bufs=CHUNKS))
+        h_psum = ctx.enter_context(tc.psum_pool(name="h_psum", bufs=1))
+        psum = ctx.enter_context(tc.psum_pool(name="psum", bufs=2))
+
+        def load_rows(rows, name):
+            raw = keep.tile([P, PACK, rows.shape[1]], F32, name=name)
+            nc.sync.dma_start(out=raw[:], in_=rows.rearrange("(p j) w -> p j w", j=PACK))
+            return raw
+
+        def interleave(copy, grouped, g0, raw, c0, c1):
+            width = c1 - c0
+            copy(
+                out=grouped[:, PACK * g0 : PACK * (g0 + width)].rearrange("p (c i t) -> p c t i", i=4, t=PACK),
+                in_=raw[:, :, c0:c1].rearrange("p t (c i) -> p c t i", i=4),
+            )
+
+        def quantize(grouped, width, name):
+            codes = keep.tile([P, width], U32, name=name + "_codes", align_bytes=64)
+            scales = keep.tile([P, width], U8, name=name + "_scales", align_bytes=64)
+            nc.vector.quantize_mx(out=codes[:].bitcast(FP8X4), scales=scales[:], in_=grouped[:])
+            return codes, scales
+
+        def load_words(z):
+            words = keep.tile([P, T], U32, name="x_words%d" % z, align_bytes=64)
+            nc.sync.dma_start(
+                out=words[:].bitcast(I32), in_=x_words[z].rearrange("p n t -> p (n t)").bitcast(I32)
+            )
+            return words
+
+        xs = keep.tile([P, T], U8, align_bytes=64)
+        w4s = keep.tile([P, N], U8, align_bytes=64)
+        nc.vector.memset(xs[:].bitcast(I32), 0)
+        nc.vector.memset(w4s[:].bitcast(I32), 0)
+        ident = keep.tile([P, P], F32)
+        make_identity(nc, ident[:])
+
+        raw_w = {}
+        raw_w[0, 0] = load_rows(w1[0:K_PASS, :], "w1a")
+        for q in range(4):
+            nc.sync.dma_start(
+                out=xs[32 * q : 32 * q + 8, :].bitcast(I32), in_=x_scales[:, 4 * q : 4 * q + 4, :].bitcast(I32)
+            )
+        offsets = keep.tile([P, S // 16], U16)
+        nc.sync.dma_start(offsets[:], offs)
+        xw = [load_words(0)]
+        raw_w[0, 1] = load_rows(w2[0:K_PASS, :], "w2a")
+        xw.append(load_words(1))
+        raw_w[1, 0] = load_rows(w1[K_PASS:K, :], "w1b")
+        raw_w[1, 1] = load_rows(w2[K_PASS:K, :], "w2b")
+        w4w = keep.tile([P, 2 * N], U8, align_bytes=64)
+        nc.sync.dma_start(out=w4w[:].bitcast(I32), in_=w4_words[0].bitcast(I32))
+        for q in range(4):
+            nc.sync.dma_start(
+                out=w4s[32 * q : 32 * q + 4, :].bitcast(I32), in_=w4_scales[0, 4 * q : 4 * q + 4, :].bitcast(I32)
+            )
+        raw_w3 = load_rows(w3, "w3")
+        raw_e = [load_rows(eT[:, a:b], "e%d" % a) for a, b in E_LOADS]
+
+        h_banks = [h_psum.tile([P, H], F32, name="h%d" % c) for c in range(CHUNKS)]
+
+        def weight_codes(raw, name, shared):
+            grouped = keep.tile([P, PACK * H], BF16, name=name + "_bf16", align_bytes=64)
+            if shared:
+                interleave(nc.vector.tensor_copy, grouped, 0, raw, 0, VECTOR_SHARE)
+                interleave(nc.scalar.copy, grouped, VECTOR_SHARE, raw, VECTOR_SHARE, H)
+            else:
+                interleave(nc.scalar.copy, grouped, 0, raw, 0, H)
+            return quantize(grouped, H, name)
+
+        picked_scales = {}
+        for z in range(2):
+            for side in range(2):
+                entries = offsets[:, side * V // 16 : (side + 1) * V // 16]
+                picked = keep.tile([P, V], U32, name="picked%d%d" % (z, side), align_bytes=64)
+                nc.vector.tensor_copy(out=picked[:], in_=xw[z][:].indirect(entries))
+                if z == 0:
+                    picked_scales[side] = keep.tile([P, V], U8, name="picked_scales%d" % side, align_bytes=64)
+                    nc.vector.tensor_copy(out=picked_scales[side][:], in_=xs[:].indirect(entries))
+                codes, scales = weight_codes(raw_w[z, side], "w%d%d" % (z, side), (z, side) == (1, 1))
+                for c in range(CHUNKS):
+                    cols = slice(c * EDGES, (c + 1) * EDGES)
+                    nc.tensor.matmul_mx(
+                        out=h_banks[c][:],
+                        lhsT=picked[:, cols].bitcast(FP8X4),
+                        lhsT_scale=picked_scales[side][4 * z : P, cols],
+                        rhs=codes[:].bitcast(FP8X4),
+                        rhs_scale=scales[:],
+                        start=(z, side) == (0, 0),
+                        stop=False,
+                    )
+
+        w3_codes, w3_scales = weight_codes(raw_w3, "w3", True)
+
+        hidden = []
+        for c in range(CHUNKS):
+            piece = max(i for i, (a, b) in enumerate(E_LOADS) if a <= c * EDGES)
+            c0 = c * EDGES - E_LOADS[piece][0]
+            grouped = keep.tile([P, PACK * EDGES], BF16, name="e%d_bf16" % c, align_bytes=64)
+            interleave(nc.vector.tensor_copy, grouped, 0, raw_e[piece], c0, c0 + EDGES)
+            e_codes, e_scales = quantize(grouped, EDGES, "e%d" % c)
+            nc.tensor.matmul_mx(
+                out=h_banks[c][:],
+                lhsT=e_codes[:].bitcast(FP8X4),
+                lhsT_scale=e_scales[:],
+                rhs=w3_codes[:].bitcast(FP8X4),
+                rhs_scale=w3_scales[:],
+                start=False,
+                stop=True,
+            )
+            h_bf16 = ring.tile([P, H], BF16, align_bytes=64)
+            nc.scalar.activation(
+                out=h_bf16[:].rearrange("v (u p e) -> v u p e", u=2, e=2),
+                in_=h_banks[c][:].rearrange("v (p u e) -> v u p e", u=2, e=2),
+                func=GELU,
+            )
+            hidden.append(h_bf16)
+
+        for c in range(CHUNKS):
+            pairs = hidden[c][:].bitcast(F32)
+            turned = psum.tile([P, 2, EDGES], F32)
+            for u in range(2):
+                nc.tensor.transpose(turned[:, u, :], pairs[:, u * P : (u + 1) * P], ident[:])
+            h_grouped = ring.tile([P, PACK * EDGES], BF16, align_bytes=64)
+            nc.vector.tensor_copy(
+                out=h_grouped[:].bitcast(F32).rearrange("p (v u) -> p v u", u=2),
+                in_=turned[:].rearrange("p u v -> p v u"),
+            )
+            h_codes, h_scales = quantize(h_grouped, EDGES, "h%d" % c)
+            acc = psum.tile([N, EDGES], F32)
+            nc.tensor.matmul_mx(
+                out=acc[:],
+                lhsT=w4w[:].bitcast(FP4X4),
+                lhsT_scale=w4s[:],
+                rhs=h_codes[:].bitcast(FP8X4),
+                rhs_scale=h_scales[:],
+                start=True,
+                stop=True,
+            )
+            result = ring.tile([N, EDGES], F32)
+            nc.scalar.copy(out=result[:], in_=acc[:])
+            nc.sync.dma_start(out=out[:, c * EDGES : (c + 1) * EDGES], in_=result[:])

@@ -21,8 +21,8 @@ PACK = 4
 K_PASS = P * PACK
 EDGES = 128
 CHUNKS = V // EDGES
+HALF = H // 2
 E_LOADS = ((0, 256), (256, 384), (384, 512))
-VECTOR_SHARE = 336
 
 
 def tile_picked_edgeup_gelu_p_kernel(
@@ -40,16 +40,21 @@ def tile_picked_edgeup_gelu_p_kernel(
             nc.sync.dma_start(out=raw[:], in_=rows.rearrange("(p j) w -> p j w", j=PACK))
             return raw
 
-        def interleave(copy, grouped, g0, raw, c0, c1):
-            width = c1 - c0
+        def interleave(copy, raw, c0, c1, name):
+            grouped = keep.tile([P, PACK * (c1 - c0)], BF16, name=name, align_bytes=64)
             copy(
-                out=grouped[:, PACK * g0 : PACK * (g0 + width)].rearrange("p (c i t) -> p c t i", i=4, t=PACK),
+                out=grouped[:].rearrange("p (c i t) -> p c t i", i=4, t=PACK),
                 in_=raw[:, :, c0:c1].rearrange("p t (c i) -> p c t i", i=4),
             )
+            return grouped
+
+        def mx_tiles(width, name, scale_tag=None):
+            codes = keep.tile([P, width], U32, name=name + "_codes", align_bytes=64)
+            scales = keep.tile([P, width], U8, name=name + "_scales", tag=scale_tag or name + "_scales", align_bytes=64)
+            return codes, scales
 
         def quantize(grouped, width, name):
-            codes = keep.tile([P, width], U32, name=name + "_codes", align_bytes=64)
-            scales = keep.tile([P, width], U8, name=name + "_scales", align_bytes=64)
+            codes, scales = mx_tiles(width, name)
             nc.vector.quantize_mx(out=codes[:].bitcast(FP8X4), scales=scales[:], in_=grouped[:])
             return codes, scales
 
@@ -60,76 +65,82 @@ def tile_picked_edgeup_gelu_p_kernel(
             )
             return words
 
-        xs = keep.tile([P, T], U8, align_bytes=64)
+        xs = keep.tile([P, T], U8, tag="xs", align_bytes=64)
         w4s = keep.tile([P, N], U8, align_bytes=64)
         nc.vector.memset(xs[:].bitcast(I32), 0)
         nc.vector.memset(w4s[:].bitcast(I32), 0)
-        ident = keep.tile([P, P], F32)
-        make_identity(nc, ident[:])
+        warm_in = keep.tile([P, 1], F32)
+        warm = keep.tile([P, 1], F32)
+        nc.vector.memset(warm_in[:], 0.0)
+        nc.scalar.activation(out=warm[:], in_=warm_in[:], func=GELU)
 
-        raw_w = {}
-        raw_w[0, 0] = load_rows(w1[0:K_PASS, :], "w1a")
+        xw = [load_words(0)]
+        offsets = keep.tile([P, S // 16], U16)
+        nc.sync.dma_start(offsets[:], offs)
         for q in range(4):
             nc.sync.dma_start(
                 out=xs[32 * q : 32 * q + 8, :].bitcast(I32), in_=x_scales[:, 4 * q : 4 * q + 4, :].bitcast(I32)
             )
-        offsets = keep.tile([P, S // 16], U16)
-        nc.sync.dma_start(offsets[:], offs)
-        xw = [load_words(0)]
-        raw_w[0, 1] = load_rows(w2[0:K_PASS, :], "w2a")
         xw.append(load_words(1))
-        raw_w[1, 0] = load_rows(w1[K_PASS:K, :], "w1b")
-        raw_w[1, 1] = load_rows(w2[K_PASS:K, :], "w2b")
+        raw_w = [load_rows(w1[0:K_PASS, :], "w1a"), load_rows(w2[0:K_PASS, :], "w2a")]
         w4w = keep.tile([P, 2 * N], U8, align_bytes=64)
         nc.sync.dma_start(out=w4w[:].bitcast(I32), in_=w4_words[0].bitcast(I32))
+        raw_w.append(load_rows(w1[K_PASS:K, :], "w1b"))
         for q in range(4):
             nc.sync.dma_start(
                 out=w4s[32 * q : 32 * q + 4, :].bitcast(I32), in_=w4_scales[0, 4 * q : 4 * q + 4, :].bitcast(I32)
             )
-        raw_w3 = load_rows(w3, "w3")
+        raw_w.append(load_rows(w2[K_PASS:K, :], "w2b"))
+        raw_w.append(load_rows(w3, "w3"))
         raw_e = [load_rows(eT[:, a:b], "e%d" % a) for a, b in E_LOADS]
+        ident = keep.tile([P, P], F32)
+        make_identity(nc, ident[:])
 
         h_banks = [h_psum.tile([P, H], F32, name="h%d" % c) for c in range(CHUNKS)]
 
-        def weight_codes(raw, name, shared):
-            grouped = keep.tile([P, PACK * H], BF16, name=name + "_bf16", align_bytes=64)
-            if shared:
-                interleave(nc.vector.tensor_copy, grouped, 0, raw, 0, VECTOR_SHARE)
-                interleave(nc.scalar.copy, grouped, VECTOR_SHARE, raw, VECTOR_SHARE, H)
-            else:
-                interleave(nc.scalar.copy, grouped, 0, raw, 0, H)
-            return quantize(grouped, H, name)
-
-        picked_scales = {}
+        picked = []
         for z in range(2):
-            for side in range(2):
-                entries = offsets[:, side * V // 16 : (side + 1) * V // 16]
-                picked = keep.tile([P, V], U32, name="picked%d%d" % (z, side), align_bytes=64)
-                nc.vector.tensor_copy(out=picked[:], in_=xw[z][:].indirect(entries))
-                if z == 0:
-                    picked_scales[side] = keep.tile([P, V], U8, name="picked_scales%d" % side, align_bytes=64)
-                    nc.vector.tensor_copy(out=picked_scales[side][:], in_=xs[:].indirect(entries))
-                codes, scales = weight_codes(raw_w[z, side], "w%d%d" % (z, side), (z, side) == (1, 1))
-                for c in range(CHUNKS):
-                    cols = slice(c * EDGES, (c + 1) * EDGES)
-                    nc.tensor.matmul_mx(
-                        out=h_banks[c][:],
-                        lhsT=picked[:, cols].bitcast(FP8X4),
-                        lhsT_scale=picked_scales[side][4 * z : P, cols],
-                        rhs=codes[:].bitcast(FP8X4),
-                        rhs_scale=scales[:],
-                        start=(z, side) == (0, 0),
-                        stop=False,
-                    )
+            words = keep.tile([P, S], U32, name="picked%d" % z, align_bytes=64)
+            nc.vector.tensor_copy(out=words[:], in_=xw[z][:].indirect(offsets[:]))
+            picked.append(words)
+        picked_scales = keep.tile([P, S], U8, align_bytes=64)
+        nc.vector.tensor_copy(out=picked_scales[:], in_=xs[:].indirect(offsets[:]))
 
-        w3_codes, w3_scales = weight_codes(raw_w3, "w3", True)
+        def weight_codes(n):
+            name = "w%d" % n
+            first = nc.scalar.copy if n == 0 else nc.vector.tensor_copy
+            parts = [
+                interleave(copy, raw_w[n], a * HALF, (a + 1) * HALF, name + "_bf16_%d" % a)
+                for a, copy in enumerate((first, nc.scalar.copy))
+            ]
+            codes, scales = mx_tiles(H, name, "xs" if n == 0 else None)
+            for a in range(2):
+                cols = slice(a * HALF, (a + 1) * HALF)
+                nc.vector.quantize_mx(out=codes[:, cols].bitcast(FP8X4), scales=scales[:, cols], in_=parts[a][:])
+            return codes, scales
+
+        for n in range(4):
+            z, side = divmod(n, 2)
+            codes, scales = weight_codes(n)
+            for c in range(CHUNKS):
+                cols = slice(side * V + c * EDGES, side * V + (c + 1) * EDGES)
+                nc.tensor.matmul_mx(
+                    out=h_banks[c][:],
+                    lhsT=picked[z][:, cols].bitcast(FP8X4),
+                    lhsT_scale=picked_scales[4 * z : P, cols],
+                    rhs=codes[:].bitcast(FP8X4),
+                    rhs_scale=scales[:],
+                    start=n == 0,
+                    stop=False,
+                )
+        w3_codes, w3_scales = weight_codes(4)
 
         hidden = []
         for c in range(CHUNKS):
             piece = max(i for i, (a, b) in enumerate(E_LOADS) if a <= c * EDGES)
             c0 = c * EDGES - E_LOADS[piece][0]
-            grouped = keep.tile([P, PACK * EDGES], BF16, name="e%d_bf16" % c, align_bytes=64)
-            interleave(nc.vector.tensor_copy, grouped, 0, raw_e[piece], c0, c0 + EDGES)
+            copy = nc.scalar.copy if c == 1 else nc.vector.tensor_copy
+            grouped = interleave(copy, raw_e[piece], c0, c0 + EDGES, "e%d_bf16" % c)
             e_codes, e_scales = quantize(grouped, EDGES, "e%d" % c)
             nc.tensor.matmul_mx(
                 out=h_banks[c][:],
@@ -141,11 +152,13 @@ def tile_picked_edgeup_gelu_p_kernel(
                 stop=True,
             )
             h_bf16 = ring.tile([P, H], BF16, align_bytes=64)
-            nc.scalar.activation(
-                out=h_bf16[:].rearrange("v (u p e) -> v u p e", u=2, e=2),
-                in_=h_banks[c][:].rearrange("v (p u e) -> v u p e", u=2, e=2),
-                func=GELU,
-            )
+            halves = [(0, 1), (1, 2)] if c == CHUNKS - 1 else [(0, 2)]
+            for u0, u1 in halves:
+                nc.scalar.activation(
+                    out=h_bf16[:].rearrange("v (u p e) -> v u p e", u=2, e=2)[:, u0:u1],
+                    in_=h_banks[c][:].rearrange("v (p u e) -> v u p e", u=2, e=2)[:, u0:u1],
+                    func=GELU,
+                )
             hidden.append(h_bf16)
 
         for c in range(CHUNKS):
@@ -154,7 +167,8 @@ def tile_picked_edgeup_gelu_p_kernel(
             for u in range(2):
                 nc.tensor.transpose(turned[:, u, :], pairs[:, u * P : (u + 1) * P], ident[:])
             h_grouped = ring.tile([P, PACK * EDGES], BF16, align_bytes=64)
-            nc.vector.tensor_copy(
+            copy_out = nc.scalar.copy if c == CHUNKS - 1 else nc.vector.tensor_copy
+            copy_out(
                 out=h_grouped[:].bitcast(F32).rearrange("p (v u) -> p v u", u=2),
                 in_=turned[:].rearrange("p u v -> p v u"),
             )

@@ -1,7 +1,6 @@
 from contextlib import ExitStack
 
 import concourse.mybir as mybir
-from concourse.masks import make_identity
 
 K, T, S, V, H, N, J = 1024, 2048, 1024, 512, 512, 128, 512
 FLOPS = 2 * (2 * K * H * V + J * H * V + H * N * V)
@@ -19,10 +18,9 @@ GELU = mybir.ActivationFunctionType.Gelu_apprx_tanh
 P = 128
 PACK = 4
 K_PASS = P * PACK
-EDGES = 128
-CHUNKS = V // EDGES
-HALF = H // 2
-E_LOADS = ((0, 256), (256, 384), (384, 512))
+EDGES = V // 2
+PIECES = (((0, EDGES),), ((0, EDGES // 2), (EDGES // 2, EDGES)))
+E_SPLIT = (128, 168)
 
 
 def tile_picked_edgeup_gelu_p_kernel(
@@ -31,22 +29,18 @@ def tile_picked_edgeup_gelu_p_kernel(
     nc = tc.nc
     with ExitStack() as ctx:
         keep = ctx.enter_context(tc.tile_pool(name="keep", bufs=1))
-        ring = ctx.enter_context(tc.tile_pool(name="ring", bufs=CHUNKS))
-        h_psum = ctx.enter_context(tc.psum_pool(name="h_psum", bufs=1))
-        psum = ctx.enter_context(tc.psum_pool(name="psum", bufs=2))
+        psum = ctx.enter_context(tc.psum_pool(name="psum", bufs=1))
 
         def load_rows(rows, name):
             raw = keep.tile([P, PACK, rows.shape[1]], F32, name=name)
             nc.sync.dma_start(out=raw[:], in_=rows.rearrange("(p j) w -> p j w", j=PACK))
             return raw
 
-        def interleave(copy, raw, c0, c1, name):
-            grouped = keep.tile([P, PACK * (c1 - c0)], BF16, name=name, align_bytes=64)
+        def interleave(copy, grouped, planes, c0, c1):
             copy(
-                out=grouped[:].rearrange("p (c i t) -> p c t i", i=4, t=PACK),
-                in_=raw[:, :, c0:c1].rearrange("p t (c i) -> p c t i", i=4),
+                out=grouped[:, PACK * c0 : PACK * c1].rearrange("p (c i t) -> p c t i", i=4, t=PACK),
+                in_=planes[:, :, c0:c1].rearrange("p t (c i) -> p c t i", i=4),
             )
-            return grouped
 
         def mx_tiles(width, name, scale_tag=None):
             codes = keep.tile([P, width], U32, name=name + "_codes", align_bytes=64)
@@ -82,21 +76,19 @@ def tile_picked_edgeup_gelu_p_kernel(
                 out=xs[32 * q : 32 * q + 8, :].bitcast(I32), in_=x_scales[:, 4 * q : 4 * q + 4, :].bitcast(I32)
             )
         xw.append(load_words(1))
-        raw_w = [load_rows(w1[0:K_PASS, :], "w1a"), load_rows(w2[0:K_PASS, :], "w2a")]
+        raw_w = [
+            load_rows(rows, "w%d" % n)
+            for n, rows in enumerate((w1[0:K_PASS, :], w2[0:K_PASS, :], w1[K_PASS:K, :], w2[K_PASS:K, :], w3))
+        ]
+        raw_e = [load_rows(eT[:, a * EDGES : (a + 1) * EDGES], "e%d" % a) for a in range(2)]
         w4w = keep.tile([P, 2 * N], U8, align_bytes=64)
         nc.sync.dma_start(out=w4w[:].bitcast(I32), in_=w4_words[0].bitcast(I32))
-        raw_w.append(load_rows(w1[K_PASS:K, :], "w1b"))
         for q in range(4):
             nc.sync.dma_start(
                 out=w4s[32 * q : 32 * q + 4, :].bitcast(I32), in_=w4_scales[0, 4 * q : 4 * q + 4, :].bitcast(I32)
             )
-        raw_w.append(load_rows(w2[K_PASS:K, :], "w2b"))
-        raw_w.append(load_rows(w3, "w3"))
-        raw_e = [load_rows(eT[:, a:b], "e%d" % a) for a, b in E_LOADS]
-        ident = keep.tile([P, P], F32)
-        make_identity(nc, ident[:])
 
-        h_banks = [h_psum.tile([P, H], F32, name="h%d" % c) for c in range(CHUNKS)]
+        banks = [[psum.tile([P, EDGES], F32, name="h%d%d" % (a, t)) for t in range(PACK)] for a in range(2)]
 
         picked = []
         for z in range(2):
@@ -109,71 +101,64 @@ def tile_picked_edgeup_gelu_p_kernel(
         def weight_codes(n):
             name = "w%d" % n
             first = nc.scalar.copy if n == 0 else nc.vector.tensor_copy
-            parts = [
-                interleave(copy, raw_w[n], a * HALF, (a + 1) * HALF, name + "_bf16_%d" % a)
-                for a, copy in enumerate((first, nc.scalar.copy))
-            ]
+            parts = []
+            for u, copy in enumerate((first, nc.scalar.copy)):
+                grouped = keep.tile([P, PACK * 2 * P], BF16, name=name + "_bf16_%d" % u, align_bytes=64)
+                copy(
+                    out=grouped[:].rearrange("p (t m j) -> p m j t", t=2, j=PACK),
+                    in_=raw_w[n][:].rearrange("p j (m t) -> p m j t", t=PACK)[:, :, :, 2 * u : 2 * u + 2],
+                )
+                parts.append(grouped)
             codes, scales = mx_tiles(H, name, "xs" if n == 0 else None)
-            for a in range(2):
-                cols = slice(a * HALF, (a + 1) * HALF)
-                nc.vector.quantize_mx(out=codes[:, cols].bitcast(FP8X4), scales=scales[:, cols], in_=parts[a][:])
+            for u in range(2):
+                cols = slice(2 * u * P, 2 * (u + 1) * P)
+                nc.vector.quantize_mx(out=codes[:, cols].bitcast(FP8X4), scales=scales[:, cols], in_=parts[u][:])
             return codes, scales
 
         for n in range(4):
             z, side = divmod(n, 2)
             codes, scales = weight_codes(n)
-            for c in range(CHUNKS):
-                cols = slice(side * V + c * EDGES, side * V + (c + 1) * EDGES)
-                nc.tensor.matmul_mx(
-                    out=h_banks[c][:],
-                    lhsT=picked[z][:, cols].bitcast(FP8X4),
-                    lhsT_scale=picked_scales[4 * z : P, cols],
-                    rhs=codes[:].bitcast(FP8X4),
-                    rhs_scale=scales[:],
-                    start=n == 0,
-                    stop=False,
-                )
+            for t in range(PACK):
+                for a in range(2):
+                    cols = slice(side * V + a * EDGES, side * V + (a + 1) * EDGES)
+                    nc.tensor.matmul_mx(
+                        out=banks[a][t][:],
+                        lhsT=codes[:, t * P : (t + 1) * P].bitcast(FP8X4),
+                        lhsT_scale=scales[:, t * P : (t + 1) * P],
+                        rhs=picked[z][:, cols].bitcast(FP8X4),
+                        rhs_scale=picked_scales[4 * z : P, cols],
+                        start=n == 0,
+                        stop=False,
+                    )
         w3_codes, w3_scales = weight_codes(4)
 
         hidden = []
-        for c in range(CHUNKS):
-            piece = max(i for i, (a, b) in enumerate(E_LOADS) if a <= c * EDGES)
-            c0 = c * EDGES - E_LOADS[piece][0]
-            copy = nc.scalar.copy if c == 1 else nc.vector.tensor_copy
-            grouped = interleave(copy, raw_e[piece], c0, c0 + EDGES, "e%d_bf16" % c)
-            e_codes, e_scales = quantize(grouped, EDGES, "e%d" % c)
-            nc.tensor.matmul_mx(
-                out=h_banks[c][:],
-                lhsT=e_codes[:].bitcast(FP8X4),
-                lhsT_scale=e_scales[:],
-                rhs=w3_codes[:].bitcast(FP8X4),
-                rhs_scale=w3_scales[:],
-                start=False,
-                stop=True,
-            )
-            h_bf16 = ring.tile([P, H], BF16, align_bytes=64)
-            halves = [(0, 1), (1, 2)] if c == CHUNKS - 1 else [(0, 2)]
-            for u0, u1 in halves:
-                nc.scalar.activation(
-                    out=h_bf16[:].rearrange("v (u p e) -> v u p e", u=2, e=2)[:, u0:u1],
-                    in_=h_banks[c][:].rearrange("v (p u e) -> v u p e", u=2, e=2)[:, u0:u1],
-                    func=GELU,
+        for a in range(2):
+            grouped = keep.tile([P, PACK * EDGES], BF16, name="e%d_bf16" % a, align_bytes=64)
+            interleave(nc.vector.tensor_copy, grouped, raw_e[a], 0, E_SPLIT[a])
+            interleave(nc.scalar.copy, grouped, raw_e[a], E_SPLIT[a], EDGES)
+            e_codes, e_scales = quantize(grouped, EDGES, "e%d" % a)
+            for t in range(PACK):
+                nc.tensor.matmul_mx(
+                    out=banks[a][t][:],
+                    lhsT=w3_codes[:, t * P : (t + 1) * P].bitcast(FP8X4),
+                    lhsT_scale=w3_scales[:, t * P : (t + 1) * P],
+                    rhs=e_codes[:].bitcast(FP8X4),
+                    rhs_scale=e_scales[:],
+                    start=False,
+                    stop=True,
                 )
-            hidden.append(h_bf16)
+            for c0, c1 in PIECES[a]:
+                planes = keep.tile([P, PACK, c1 - c0], BF16, name="h%d_%d" % (a, c0))
+                for t in range(PACK):
+                    nc.scalar.activation(out=planes[:, t, :], in_=banks[a][t][:, c0:c1], func=GELU)
+                hidden.append((a * EDGES + c0, c1 - c0, planes))
 
-        for c in range(CHUNKS):
-            pairs = hidden[c][:].bitcast(F32)
-            turned = psum.tile([P, 2, EDGES], F32)
-            for u in range(2):
-                nc.tensor.transpose(turned[:, u, :], pairs[:, u * P : (u + 1) * P], ident[:])
-            h_grouped = ring.tile([P, PACK * EDGES], BF16, align_bytes=64)
-            copy_out = nc.scalar.copy if c == CHUNKS - 1 else nc.vector.tensor_copy
-            copy_out(
-                out=h_grouped[:].bitcast(F32).rearrange("p (v u) -> p v u", u=2),
-                in_=turned[:].rearrange("p u v -> p v u"),
-            )
-            h_codes, h_scales = quantize(h_grouped, EDGES, "h%d" % c)
-            acc = psum.tile([N, EDGES], F32)
+        for i, (first, width, planes) in enumerate(hidden):
+            grouped = keep.tile([P, PACK * width], BF16, name="h_bf16_%d" % i, align_bytes=64)
+            interleave(nc.vector.tensor_copy, grouped, planes, 0, width)
+            h_codes, h_scales = quantize(grouped, width, "h%d" % i)
+            acc = psum.tile([N, width], F32, name="acc%d" % i, tag="h0%d" % i)
             nc.tensor.matmul_mx(
                 out=acc[:],
                 lhsT=w4w[:].bitcast(FP4X4),
@@ -183,6 +168,6 @@ def tile_picked_edgeup_gelu_p_kernel(
                 start=True,
                 stop=True,
             )
-            result = ring.tile([N, EDGES], F32)
+            result = keep.tile([N, width], F32, name="result%d" % i)
             nc.scalar.copy(out=result[:], in_=acc[:])
-            nc.sync.dma_start(out=out[:, c * EDGES : (c + 1) * EDGES], in_=result[:])
+            nc.sync.dma_start(out=out[:, first : first + width], in_=result[:])

@@ -19,8 +19,7 @@ P = 128
 PACK = 4
 K_PASS = P * PACK
 EDGES = V // 2
-PIECES = (((0, EDGES),), ((0, EDGES // 2), (EDGES // 2, EDGES)))
-E_SPLIT = (128, 168)
+QUARTER = EDGES // 2
 
 
 def tile_picked_edgeup_gelu_p_kernel(
@@ -77,10 +76,12 @@ def tile_picked_edgeup_gelu_p_kernel(
             )
         xw.append(load_words(1))
         raw_w = [
-            load_rows(rows, "w%d" % n)
-            for n, rows in enumerate((w1[0:K_PASS, :], w2[0:K_PASS, :], w1[K_PASS:K, :], w2[K_PASS:K, :], w3))
+            load_rows(rows, "w%d" % n) for n, rows in enumerate((w1[0:K_PASS, :], w2[0:K_PASS, :], w1[K_PASS:K, :]))
         ]
-        raw_e = [load_rows(eT[:, a * EDGES : (a + 1) * EDGES], "e%d" % a) for a in range(2)]
+        raw_e = [load_rows(eT[:, 0:EDGES], "e0")]
+        raw_w.append(load_rows(w2[K_PASS:K, :], "w3"))
+        raw_w.append(load_rows(w3, "w4"))
+        raw_e.append(load_rows(eT[:, EDGES:V], "e1"))
         w4w = keep.tile([P, 2 * N], U8, align_bytes=64)
         nc.sync.dma_start(out=w4w[:].bitcast(I32), in_=w4_words[0].bitcast(I32))
         for q in range(4):
@@ -95,28 +96,38 @@ def tile_picked_edgeup_gelu_p_kernel(
             words = keep.tile([P, S], U32, name="picked%d" % z, align_bytes=64)
             nc.vector.tensor_copy(out=words[:], in_=xw[z][:].indirect(offsets[:]))
             picked.append(words)
-        picked_scales = keep.tile([P, S], U8, align_bytes=64)
-        nc.vector.tensor_copy(out=picked_scales[:], in_=xs[:].indirect(offsets[:]))
+            if z == 0:
+                picked_scales = keep.tile([P, S], U8, align_bytes=64)
+                nc.vector.tensor_copy(out=picked_scales[:], in_=xs[:].indirect(offsets[:]))
 
         def weight_codes(n):
             name = "w%d" % n
+            parts = [
+                keep.tile([P, PACK * 2 * P], BF16, name=name + "_bf16_%d" % u, align_bytes=64) for u in range(2)
+            ]
             first = nc.scalar.copy if n == 0 else nc.vector.tensor_copy
-            parts = []
             for u, copy in enumerate((first, nc.scalar.copy)):
-                grouped = keep.tile([P, PACK * 2 * P], BF16, name=name + "_bf16_%d" % u, align_bytes=64)
                 copy(
-                    out=grouped[:].rearrange("p (t m j) -> p m j t", t=2, j=PACK),
+                    out=parts[u][:].rearrange("p (t m j) -> p m j t", t=2, j=PACK),
                     in_=raw_w[n][:].rearrange("p j (m t) -> p m j t", t=PACK)[:, :, :, 2 * u : 2 * u + 2],
                 )
-                parts.append(grouped)
             codes, scales = mx_tiles(H, name, "xs" if n == 0 else None)
             for u in range(2):
                 cols = slice(2 * u * P, 2 * (u + 1) * P)
                 nc.vector.quantize_mx(out=codes[:, cols].bitcast(FP8X4), scales=scales[:, cols], in_=parts[u][:])
             return codes, scales
 
+        def edge_codes(a):
+            grouped = keep.tile([P, PACK * EDGES], BF16, name="e%d_bf16" % a, align_bytes=64)
+            interleave(nc.vector.tensor_copy, grouped, raw_e[a], 0, QUARTER)
+            interleave(nc.scalar.copy, grouped, raw_e[a], QUARTER, EDGES)
+            return quantize(grouped, EDGES, "e%d" % a)
+
+        e_mx = []
         for n in range(4):
             z, side = divmod(n, 2)
+            if n == 3:
+                e_mx.append(edge_codes(0))
             codes, scales = weight_codes(n)
             for t in range(PACK):
                 for a in range(2):
@@ -131,13 +142,11 @@ def tile_picked_edgeup_gelu_p_kernel(
                         stop=False,
                     )
         w3_codes, w3_scales = weight_codes(4)
+        e_mx.append(edge_codes(1))
 
         hidden = []
         for a in range(2):
-            grouped = keep.tile([P, PACK * EDGES], BF16, name="e%d_bf16" % a, align_bytes=64)
-            interleave(nc.vector.tensor_copy, grouped, raw_e[a], 0, E_SPLIT[a])
-            interleave(nc.scalar.copy, grouped, raw_e[a], E_SPLIT[a], EDGES)
-            e_codes, e_scales = quantize(grouped, EDGES, "e%d" % a)
+            e_codes, e_scales = e_mx[a]
             for t in range(PACK):
                 nc.tensor.matmul_mx(
                     out=banks[a][t][:],
@@ -148,17 +157,20 @@ def tile_picked_edgeup_gelu_p_kernel(
                     start=False,
                     stop=True,
                 )
-            for c0, c1 in PIECES[a]:
-                planes = keep.tile([P, PACK, c1 - c0], BF16, name="h%d_%d" % (a, c0))
+            width = (EDGES, QUARTER)[a]
+            for b in range(EDGES // width):
+                planes = keep.tile([P, PACK, width], BF16, name="h%d%d_planes" % (a, b), align_bytes=64)
                 for t in range(PACK):
-                    nc.scalar.activation(out=planes[:, t, :], in_=banks[a][t][:, c0:c1], func=GELU)
-                hidden.append((a * EDGES + c0, c1 - c0, planes))
+                    nc.scalar.activation(
+                        out=planes[:, t, :], in_=banks[a][t][:, b * width : (b + 1) * width], func=GELU
+                    )
+                hidden.append(planes)
 
-        for i, (first, width, planes) in enumerate(hidden):
-            grouped = keep.tile([P, PACK * width], BF16, name="h_bf16_%d" % i, align_bytes=64)
-            interleave(nc.vector.tensor_copy, grouped, planes, 0, width)
-            h_codes, h_scales = quantize(grouped, width, "h%d" % i)
-            acc = psum.tile([N, width], F32, name="acc%d" % i, tag="h0%d" % i)
+        def second_product(grouped, first, width, codes_tag, bank_tag, copy):
+            h_codes = keep.tile([P, width], U32, name="h%d_codes" % first, tag=codes_tag, align_bytes=64)
+            h_scales = keep.tile([P, width], U8, name="h%d_scales" % first, align_bytes=64)
+            nc.vector.quantize_mx(out=h_codes[:].bitcast(FP8X4), scales=h_scales[:], in_=grouped)
+            acc = psum.tile([N, width], F32, name="acc%d" % first, tag=bank_tag)
             nc.tensor.matmul_mx(
                 out=acc[:],
                 lhsT=w4w[:].bitcast(FP4X4),
@@ -168,6 +180,21 @@ def tile_picked_edgeup_gelu_p_kernel(
                 start=True,
                 stop=True,
             )
-            result = keep.tile([N, width], F32, name="result%d" % i)
-            nc.scalar.copy(out=result[:], in_=acc[:])
+            result = keep.tile([N, width], F32, name="result%d" % first)
+            copy(out=result[:], in_=acc[:])
             nc.sync.dma_start(out=out[:, first : first + width], in_=result[:])
+
+        def weave(planes, grouped):
+            nc.vector.tensor_copy(
+                out=grouped.rearrange("p (c i t) -> p c t i", i=4, t=PACK),
+                in_=planes[:].rearrange("p t (c i) -> p c t i", i=4),
+            )
+
+        early = keep.tile([P, PACK * EDGES], BF16, align_bytes=64)
+        weave(hidden[0], early[:])
+        second_product(early[:], 0, EDGES, "h0_codes", "h00", nc.scalar.copy)
+        late = [keep.tile([P, PACK * QUARTER], BF16, name="late%d" % b, align_bytes=64) for b in range(2)]
+        weave(hidden[1], late[0][:])
+        weave(hidden[2], late[1][:])
+        second_product(late[0][:], EDGES, QUARTER, "h11_planes", "h01", nc.scalar.copy)
+        second_product(late[1][:], EDGES + QUARTER, QUARTER, "h3_codes", "h02", nc.vector.tensor_copy)

@@ -60,7 +60,7 @@ def tile_picked_edgeup_gelu_p_kernel(
 
         xs = keep.tile([P, T], U8, tag="xs", align_bytes=64)
         w4s = keep.tile([P, N], U8, align_bytes=64)
-        nc.vector.memset(xs[:].bitcast(I32), 0)
+        nc.gpsimd.memset(xs[:].bitcast(I32), 0)
         nc.vector.memset(w4s[:].bitcast(I32), 0)
         warm_in = keep.tile([P, 1], F32)
         warm = keep.tile([P, 1], F32)
@@ -71,7 +71,7 @@ def tile_picked_edgeup_gelu_p_kernel(
         offsets = keep.tile([P, S // 16], U16)
         nc.sync.dma_start(offsets[:], offs)
         for q in range(4):
-            nc.sync.dma_start(
+            nc.gpsimd.dma_start(
                 out=xs[32 * q : 32 * q + 8, :].bitcast(I32), in_=x_scales[:, 4 * q : 4 * q + 4, :].bitcast(I32)
             )
         xw.append(load_words(1))
@@ -96,9 +96,8 @@ def tile_picked_edgeup_gelu_p_kernel(
             words = keep.tile([P, S], U32, name="picked%d" % z, align_bytes=64)
             nc.vector.tensor_copy(out=words[:], in_=xw[z][:].indirect(offsets[:]))
             picked.append(words)
-            if z == 0:
-                picked_scales = keep.tile([P, S], U8, align_bytes=64)
-                nc.vector.tensor_copy(out=picked_scales[:], in_=xs[:].indirect(offsets[:]))
+        picked_scales = keep.tile([P, S], U8, align_bytes=64)
+        nc.vector.tensor_copy(out=picked_scales[:], in_=xs[:].indirect(offsets[:]))
 
         def weight_codes(n):
             name = "w%d" % n

@@ -71,7 +71,8 @@ def tile_picked_edgeup_gelu_p_kernel(
         offsets = keep.tile([P, S // 16], U16)
         nc.sync.dma_start(offsets[:], offs)
         for q in range(4):
-            nc.gpsimd.dma_start(
+            queue = nc.sync if q < 2 else nc.gpsimd
+            queue.dma_start(
                 out=xs[32 * q : 32 * q + 8, :].bitcast(I32), in_=x_scales[:, 4 * q : 4 * q + 4, :].bitcast(I32)
             )
         xw.append(load_words(1))

@@ -35,12 +35,6 @@ def tile_picked_edgeup_gelu_p_kernel(
             nc.sync.dma_start(out=raw[:], in_=rows.rearrange("(p j) w -> p j w", j=PACK))
             return raw
 
-        def interleave(copy, grouped, planes, c0, c1):
-            copy(
-                out=grouped[:, PACK * c0 : PACK * c1].rearrange("p (c i t) -> p c t i", i=4, t=PACK),
-                in_=planes[:, :, c0:c1].rearrange("p t (c i) -> p c t i", i=4),
-            )
-
         def mx_tiles(width, name, scale_tag=None):
             codes = keep.tile([P, width], U32, name=name + "_codes", align_bytes=64)
             scales = keep.tile([P, width], U8, name=name + "_scales", tag=scale_tag or name + "_scales", align_bytes=64)
@@ -77,12 +71,10 @@ def tile_picked_edgeup_gelu_p_kernel(
             )
         xw.append(load_words(1))
         raw_w = [
-            load_rows(rows, "w%d" % n) for n, rows in enumerate((w1[0:K_PASS, :], w2[0:K_PASS, :], w1[K_PASS:K, :]))
+            load_rows(rows, "w%d" % n)
+            for n, rows in enumerate((w1[0:K_PASS, :], w2[0:K_PASS, :], w3, w1[K_PASS:K, :], w2[K_PASS:K, :]))
         ]
-        raw_e = [load_rows(eT[:, 0:EDGES], "e0")]
-        raw_w.append(load_rows(w2[K_PASS:K, :], "w3"))
-        raw_w.append(load_rows(w3, "w4"))
-        raw_e.append(load_rows(eT[:, EDGES:V], "e1"))
+        raw_e = [load_rows(eT[:, a * EDGES : (a + 1) * EDGES], "e%d" % a) for a in range(2)]
         w4w = keep.tile([P, 2 * N], U8, align_bytes=64)
         nc.sync.dma_start(out=w4w[:].bitcast(I32), in_=w4_words[0].bitcast(I32))
         for q in range(4):
@@ -90,7 +82,7 @@ def tile_picked_edgeup_gelu_p_kernel(
                 out=w4s[32 * q : 32 * q + 4, :].bitcast(I32), in_=w4_scales[0, 4 * q : 4 * q + 4, :].bitcast(I32)
             )
 
-        banks = [[psum.tile([P, EDGES], F32, name="h%d%d" % (a, t)) for t in range(PACK)] for a in range(2)]
+        banks = [psum.tile([P, PACK * QUARTER], F32, name="h%d" % q) for q in range(4)]
 
         picked = []
         for z in range(2):
@@ -117,60 +109,78 @@ def tile_picked_edgeup_gelu_p_kernel(
                 nc.vector.quantize_mx(out=codes[:, cols].bitcast(FP8X4), scales=scales[:, cols], in_=parts[u][:])
             return codes, scales
 
-        def edge_codes(a):
-            grouped = keep.tile([P, PACK * EDGES], BF16, name="e%d_bf16" % a, align_bytes=64)
-            interleave(nc.vector.tensor_copy, grouped, raw_e[a], 0, QUARTER)
-            interleave(nc.scalar.copy, grouped, raw_e[a], QUARTER, EDGES)
-            return quantize(grouped, EDGES, "e%d" % a)
+        def node_pass(weight, z, side, q, t, start):
+            codes, scales = weight
+            cols = slice(side * V + q * QUARTER, side * V + (q + 1) * QUARTER)
+            nc.tensor.matmul_mx(
+                out=banks[q][:, t * QUARTER : (t + 1) * QUARTER],
+                lhsT=codes[:, t * P : (t + 1) * P].bitcast(FP8X4),
+                lhsT_scale=scales[:, t * P : (t + 1) * P],
+                rhs=picked[z][:, cols].bitcast(FP8X4),
+                rhs_scale=picked_scales[4 * z : P, cols],
+                start=start,
+                stop=False,
+            )
 
-        e_mx = []
-        for n in range(4):
-            z, side = divmod(n, 2)
-            if n == 3:
-                e_mx.append(edge_codes(0))
-            codes, scales = weight_codes(n)
+        for side in range(2):
+            weight = weight_codes(side)
             for t in range(PACK):
-                for a in range(2):
-                    cols = slice(side * V + a * EDGES, side * V + (a + 1) * EDGES)
-                    nc.tensor.matmul_mx(
-                        out=banks[a][t][:],
-                        lhsT=codes[:, t * P : (t + 1) * P].bitcast(FP8X4),
-                        lhsT_scale=scales[:, t * P : (t + 1) * P],
-                        rhs=picked[z][:, cols].bitcast(FP8X4),
-                        rhs_scale=picked_scales[4 * z : P, cols],
-                        start=n == 0,
-                        stop=False,
-                    )
-        w3_codes, w3_scales = weight_codes(4)
-        e_mx.append(edge_codes(1))
+                for q in range(4):
+                    node_pass(weight, 0, side, q, t, side == 0 and t == 0)
+        w3_codes, w3_scales = weight_codes(2)
+        weight = weight_codes(3)
+        for t in range(PACK):
+            for q in range(4):
+                node_pass(weight, 1, 0, q, t, False)
+        last_weight = weight_codes(4)
 
-        hidden = []
+        hidden = [
+            keep.tile([P, PACK * width], BF16, name="hidden%d" % n, align_bytes=64)
+            for n, width in enumerate((EDGES, QUARTER, QUARTER))
+        ]
+        hidden_of = (
+            hidden[0][:, 0 : PACK * QUARTER],
+            hidden[0][:, PACK * QUARTER : PACK * EDGES],
+            hidden[1][:],
+            hidden[2][:],
+        )
         for a in range(2):
-            e_codes, e_scales = e_mx[a]
-            for t in range(PACK):
-                nc.tensor.matmul_mx(
-                    out=banks[a][t][:],
-                    lhsT=w3_codes[:, t * P : (t + 1) * P].bitcast(FP8X4),
-                    lhsT_scale=w3_scales[:, t * P : (t + 1) * P],
-                    rhs=e_codes[:].bitcast(FP8X4),
-                    rhs_scale=e_scales[:],
-                    start=False,
-                    stop=True,
-                )
-            width = (EDGES, QUARTER)[a]
-            for b in range(EDGES // width):
-                planes = keep.tile([P, PACK, width], BF16, name="h%d%d_planes" % (a, b), align_bytes=64)
+            for q in (2 * a, 2 * a + 1):
                 for t in range(PACK):
-                    nc.scalar.activation(
-                        out=planes[:, t, :], in_=banks[a][t][:, b * width : (b + 1) * width], func=GELU
+                    node_pass(last_weight, 1, 1, q, t, False)
+            staged = []
+            for b in range(2):
+                grouped = keep.tile([P, PACK * QUARTER], BF16, name="e%d%d_bf16" % (a, b), align_bytes=64)
+                copy = nc.scalar.copy if (a, b) == (0, 0) else nc.vector.tensor_copy
+                copy(
+                    out=grouped[:].rearrange("p (c i t) -> p c t i", i=4, t=PACK),
+                    in_=raw_e[a][:, :, b * QUARTER : (b + 1) * QUARTER].rearrange("p t (c i) -> p c t i", i=4),
+                )
+                staged.append(grouped)
+            e_mx = [quantize(staged[b], QUARTER, "e%d%d" % (a, b)) for b in range(2)]
+            for b in range(2):
+                q = 2 * a + b
+                e_codes, e_scales = e_mx[b]
+                for t in range(PACK):
+                    nc.tensor.matmul_mx(
+                        out=banks[q][:, t * QUARTER : (t + 1) * QUARTER],
+                        lhsT=w3_codes[:, t * P : (t + 1) * P].bitcast(FP8X4),
+                        lhsT_scale=w3_scales[:, t * P : (t + 1) * P],
+                        rhs=e_codes[:].bitcast(FP8X4),
+                        rhs_scale=e_scales[:],
+                        start=False,
+                        stop=t == PACK - 1,
                     )
-                hidden.append(planes)
+                nc.scalar.activation(
+                    out=hidden_of[q].rearrange("p (v t) -> p v t", t=PACK),
+                    in_=banks[q][:].rearrange("p (t v) -> p v t", t=PACK),
+                    func=GELU,
+                )
 
-        def second_product(grouped, first, width, codes_tag, bank_tag, copy):
-            h_codes = keep.tile([P, width], U32, name="h%d_codes" % first, tag=codes_tag, align_bytes=64)
-            h_scales = keep.tile([P, width], U8, name="h%d_scales" % first, align_bytes=64)
-            nc.vector.quantize_mx(out=h_codes[:].bitcast(FP8X4), scales=h_scales[:], in_=grouped)
-            acc = psum.tile([N, width], F32, name="acc%d" % first, tag=bank_tag)
+        first = 0
+        for n, width in enumerate((EDGES, QUARTER, QUARTER)):
+            h_codes, h_scales = quantize(hidden[n], width, "h%d" % n)
+            acc = psum.tile([N, width], F32, name="acc%d" % n)
             nc.tensor.matmul_mx(
                 out=acc[:],
                 lhsT=w4w[:].bitcast(FP4X4),
@@ -180,21 +190,8 @@ def tile_picked_edgeup_gelu_p_kernel(
                 start=True,
                 stop=True,
             )
-            result = keep.tile([N, width], F32, name="result%d" % first)
+            result = keep.tile([N, width], F32, name="result%d" % n)
+            copy = nc.scalar.copy if n == 2 else nc.vector.tensor_copy
             copy(out=result[:], in_=acc[:])
             nc.sync.dma_start(out=out[:, first : first + width], in_=result[:])
-
-        def weave(planes, grouped):
-            nc.vector.tensor_copy(
-                out=grouped.rearrange("p (c i t) -> p c t i", i=4, t=PACK),
-                in_=planes[:].rearrange("p t (c i) -> p c t i", i=4),
-            )
-
-        early = keep.tile([P, PACK * EDGES], BF16, align_bytes=64)
-        weave(hidden[0], early[:])
-        second_product(early[:], 0, EDGES, "h0_codes", "h00", nc.scalar.copy)
-        late = [keep.tile([P, PACK * QUARTER], BF16, name="late%d" % b, align_bytes=64) for b in range(2)]
-        weave(hidden[1], late[0][:])
-        weave(hidden[2], late[1][:])
-        second_product(late[0][:], EDGES, QUARTER, "h11_planes", "h01", nc.scalar.copy)
-        second_product(late[1][:], EDGES + QUARTER, QUARTER, "h3_codes", "h02", nc.vector.tensor_copy)
+            first = first + width

@@ -56,10 +56,6 @@ def tile_picked_edgeup_gelu_p_kernel(
         w4s = keep.tile([P, N], U8, align_bytes=64)
         nc.gpsimd.memset(xs[:].bitcast(I32), 0)
         nc.vector.memset(w4s[:].bitcast(I32), 0)
-        warm_in = keep.tile([P, 1], F32)
-        warm = keep.tile([P, 1], F32)
-        nc.vector.memset(warm_in[:], 0.0)
-        nc.scalar.activation(out=warm[:], in_=warm_in[:], func=GELU)
 
         xw = [load_words(0)]
         offsets = keep.tile([P, S // 16], U16)

@@ -60,9 +60,14 @@ def tile_picked_edgeup_gelu_p_kernel(
         xw = [load_words(0)]
         offsets = keep.tile([P, S // 16], U16)
         nc.sync.dma_start(offsets[:], offs)
-        for q in range(4):
-            queue = nc.sync if q < 2 else nc.gpsimd
-            queue.dma_start(
+        for q in range(2):
+            for z in range(2):
+                nc.sync.dma_start(
+                    out=xs[32 * q + 4 * z : 32 * q + 4 * z + 4, :].bitcast(I32),
+                    in_=x_scales[z, 4 * q : 4 * q + 4, :].bitcast(I32),
+                )
+        for q in range(2, 4):
+            nc.gpsimd.dma_start(
                 out=xs[32 * q : 32 * q + 8, :].bitcast(I32), in_=x_scales[:, 4 * q : 4 * q + 4, :].bitcast(I32)
             )
         xw.append(load_words(1))

@@ -20,6 +20,7 @@ PACK = 4
 K_PASS = P * PACK
 EDGES = V // 2
 QUARTER = EDGES // 2
+VECTOR_COLUMNS = 32
 
 
 def tile_picked_edgeup_gelu_p_kernel(
@@ -73,9 +74,15 @@ def tile_picked_edgeup_gelu_p_kernel(
         xw.append(load_words(1))
         raw_w = [
             load_rows(rows, "w%d" % n)
-            for n, rows in enumerate((w1[0:K_PASS, :], w2[0:K_PASS, :], w3, w1[K_PASS:K, :], w2[K_PASS:K, :]))
+            for n, rows in enumerate((w3, w1[0:K_PASS, :], w2[0:K_PASS, :], w1[K_PASS:K, :], w2[K_PASS:K, :]))
         ]
-        raw_e = [load_rows(eT[:, a * EDGES : (a + 1) * EDGES], "e%d" % a) for a in range(2)]
+        raw_e = keep.tile([P, PACK * V], F32)
+        e_flat = eT.rearrange("(p j) v -> p (j v)", j=PACK)
+        e_rows = eT.rearrange("(p j) v -> p j v", j=PACK)
+        raw_rows = raw_e[:].rearrange("p (j v) -> p j v", j=PACK)
+        nc.sync.dma_start(out=raw_e[:, 0 : V + EDGES], in_=e_flat[:, 0 : V + EDGES])
+        nc.sync.dma_start(out=raw_rows[:, 2:PACK, 0:EDGES], in_=e_rows[:, 2:PACK, 0:EDGES])
+        nc.sync.dma_start(out=raw_rows[:, 1:PACK, EDGES:V], in_=e_rows[:, 1:PACK, EDGES:V])
         w4w = keep.tile([P, 2 * N], U8, align_bytes=64)
         nc.sync.dma_start(out=w4w[:].bitcast(I32), in_=w4_words[0].bitcast(I32))
         for q in range(4):
@@ -98,42 +105,41 @@ def tile_picked_edgeup_gelu_p_kernel(
             parts = [
                 keep.tile([P, PACK * 2 * P], BF16, name=name + "_bf16_%d" % u, align_bytes=64) for u in range(2)
             ]
-            first = nc.scalar.copy if n == 0 else nc.vector.tensor_copy
-            for u, copy in enumerate((first, nc.scalar.copy)):
+
+            def cast(copy, u, cols):
                 copy(
-                    out=parts[u][:].rearrange("p (t m j) -> p m j t", t=2, j=PACK),
-                    in_=raw_w[n][:].rearrange("p j (m t) -> p m j t", t=PACK)[:, :, :, 2 * u : 2 * u + 2],
+                    out=parts[u][:].rearrange("p (t m j) -> p m j t", t=2, j=PACK)[:, cols],
+                    in_=raw_w[n][:].rearrange("p j (m t) -> p m j t", t=PACK)[:, cols, :, 2 * u : 2 * u + 2],
                 )
+
+            cast(nc.scalar.copy if n == 0 else nc.vector.tensor_copy, 0, slice(0, P))
+            if n == len(raw_w) - 1:
+                cast(nc.vector.tensor_copy, 1, slice(0, VECTOR_COLUMNS))
+                cast(nc.scalar.copy, 1, slice(VECTOR_COLUMNS, P))
+            else:
+                cast(nc.scalar.copy, 1, slice(0, P))
             codes, scales = mx_tiles(H, name, "xs" if n == 0 else None)
             for u in range(2):
                 cols = slice(2 * u * P, 2 * (u + 1) * P)
                 nc.vector.quantize_mx(out=codes[:, cols].bitcast(FP8X4), scales=scales[:, cols], in_=parts[u][:])
             return codes, scales
 
-        def node_pass(weight, z, side, q, t, start):
-            codes, scales = weight
-            cols = slice(side * V + q * QUARTER, side * V + (q + 1) * QUARTER)
-            nc.tensor.matmul_mx(
-                out=banks[q][:, t * QUARTER : (t + 1) * QUARTER],
-                lhsT=codes[:, t * P : (t + 1) * P].bitcast(FP8X4),
-                lhsT_scale=scales[:, t * P : (t + 1) * P],
-                rhs=picked[z][:, cols].bitcast(FP8X4),
-                rhs_scale=picked_scales[4 * z : P, cols],
-                start=start,
-                stop=False,
-            )
-
-        for side in range(2):
-            weight = weight_codes(side)
+        w3_codes, w3_scales = weight_codes(0)
+        for n in range(1, len(raw_w)):
+            z, side = divmod(n - 1, 2)
+            codes, scales = weight_codes(n)
             for t in range(PACK):
                 for q in range(4):
-                    node_pass(weight, 0, side, q, t, side == 0 and t == 0)
-        w3_codes, w3_scales = weight_codes(2)
-        weight = weight_codes(3)
-        for t in range(PACK):
-            for q in range(4):
-                node_pass(weight, 1, 0, q, t, False)
-        last_weight = weight_codes(4)
+                    cols = slice(side * V + q * QUARTER, side * V + (q + 1) * QUARTER)
+                    nc.tensor.matmul_mx(
+                        out=banks[q][:, t * QUARTER : (t + 1) * QUARTER],
+                        lhsT=codes[:, t * P : (t + 1) * P].bitcast(FP8X4),
+                        lhsT_scale=scales[:, t * P : (t + 1) * P],
+                        rhs=picked[z][:, cols].bitcast(FP8X4),
+                        rhs_scale=picked_scales[4 * z : P, cols],
+                        start=n == 1 and t == 0,
+                        stop=False,
+                    )
 
         hidden = [
             keep.tile([P, PACK * width], BF16, name="hidden%d" % n, align_bytes=64)
@@ -146,19 +152,15 @@ def tile_picked_edgeup_gelu_p_kernel(
             hidden[2][:],
         )
         for a in range(2):
-            for q in (2 * a, 2 * a + 1):
-                for t in range(PACK):
-                    node_pass(last_weight, 1, 1, q, t, False)
             staged = []
-            for b in range(2):
-                grouped = keep.tile([P, PACK * QUARTER], BF16, name="e%d%d_bf16" % (a, b), align_bytes=64)
-                copy = nc.scalar.copy if (a, b) == (0, 0) else nc.vector.tensor_copy
-                copy(
+            for q in (2 * a, 2 * a + 1):
+                grouped = keep.tile([P, PACK * QUARTER], BF16, name="e%d_bf16" % q, align_bytes=64)
+                nc.vector.tensor_copy(
                     out=grouped[:].rearrange("p (c i t) -> p c t i", i=4, t=PACK),
-                    in_=raw_e[a][:, :, b * QUARTER : (b + 1) * QUARTER].rearrange("p t (c i) -> p c t i", i=4),
+                    in_=raw_rows[:, :, q * QUARTER : (q + 1) * QUARTER].rearrange("p t (c i) -> p c t i", i=4),
                 )
                 staged.append(grouped)
-            e_mx = [quantize(staged[b], QUARTER, "e%d%d" % (a, b)) for b in range(2)]
+            e_mx = [quantize(staged[b], QUARTER, "e%d" % (2 * a + b)) for b in range(2)]
             for b in range(2):
                 q = 2 * a + b
                 e_codes, e_scales = e_mx[b]

@@ -21,6 +21,7 @@ K_PASS = P * PACK
 EDGES = V // 2
 QUARTER = EDGES // 2
 VECTOR_COLUMNS = 32
+VECTOR_EDGES = (88, 88, 64, 128)
 
 
 def tile_picked_edgeup_gelu_p_kernel(
@@ -57,6 +58,10 @@ def tile_picked_edgeup_gelu_p_kernel(
         w4s = keep.tile([P, N], U8, align_bytes=64)
         nc.gpsimd.memset(xs[:].bitcast(I32), 0)
         nc.vector.memset(w4s[:].bitcast(I32), 0)
+
+        warm = keep.tile([P, 2], F32)
+        nc.vector.memset(warm[:], 0.0)
+        nc.scalar.activation(out=warm[:, 1:2], in_=warm[:, 0:1], func=GELU)
 
         xw = [load_words(0)]
         offsets = keep.tile([P, S // 16], U16)
@@ -112,7 +117,7 @@ def tile_picked_edgeup_gelu_p_kernel(
                     in_=raw_w[n][:].rearrange("p j (m t) -> p m j t", t=PACK)[:, cols, :, 2 * u : 2 * u + 2],
                 )
 
-            cast(nc.scalar.copy if n == 0 else nc.vector.tensor_copy, 0, slice(0, P))
+            cast(nc.scalar.copy if n < 2 else nc.vector.tensor_copy, 0, slice(0, P))
             if n == len(raw_w) - 1:
                 cast(nc.vector.tensor_copy, 1, slice(0, VECTOR_COLUMNS))
                 cast(nc.scalar.copy, 1, slice(VECTOR_COLUMNS, P))
@@ -124,22 +129,27 @@ def tile_picked_edgeup_gelu_p_kernel(
                 nc.vector.quantize_mx(out=codes[:, cols].bitcast(FP8X4), scales=scales[:, cols], in_=parts[u][:])
             return codes, scales
 
-        w3_codes, w3_scales = weight_codes(0)
-        for n in range(1, len(raw_w)):
+        def node_pass(weight, n, q, t):
             z, side = divmod(n - 1, 2)
-            codes, scales = weight_codes(n)
-            for t in range(PACK):
+            codes, scales = weight
+            cols = slice(side * V + q * QUARTER, side * V + (q + 1) * QUARTER)
+            nc.tensor.matmul_mx(
+                out=banks[q][:, t * QUARTER : (t + 1) * QUARTER],
+                lhsT=codes[:, t * P : (t + 1) * P].bitcast(FP8X4),
+                lhsT_scale=scales[:, t * P : (t + 1) * P],
+                rhs=picked[z][:, cols].bitcast(FP8X4),
+                rhs_scale=picked_scales[4 * z : P, cols],
+                start=n == 1 and t == 0,
+                stop=False,
+            )
+
+        w3_codes, w3_scales = weight_codes(0)
+        last = len(raw_w) - 1
+        for n in range(1, last + 1):
+            weight = weight_codes(n)
+            for t in range(PACK if n < last else 2):
                 for q in range(4):
-                    cols = slice(side * V + q * QUARTER, side * V + (q + 1) * QUARTER)
-                    nc.tensor.matmul_mx(
-                        out=banks[q][:, t * QUARTER : (t + 1) * QUARTER],
-                        lhsT=codes[:, t * P : (t + 1) * P].bitcast(FP8X4),
-                        lhsT_scale=scales[:, t * P : (t + 1) * P],
-                        rhs=picked[z][:, cols].bitcast(FP8X4),
-                        rhs_scale=picked_scales[4 * z : P, cols],
-                        start=n == 1 and t == 0,
-                        stop=False,
-                    )
+                    node_pass(weight, n, q, t)
 
         hidden = [
             keep.tile([P, PACK * width], BF16, name="hidden%d" % n, align_bytes=64)
@@ -155,15 +165,25 @@ def tile_picked_edgeup_gelu_p_kernel(
             staged = []
             for q in (2 * a, 2 * a + 1):
                 grouped = keep.tile([P, PACK * QUARTER], BF16, name="e%d_bf16" % q, align_bytes=64)
-                nc.vector.tensor_copy(
-                    out=grouped[:].rearrange("p (c i t) -> p c t i", i=4, t=PACK),
-                    in_=raw_rows[:, :, q * QUARTER : (q + 1) * QUARTER].rearrange("p t (c i) -> p c t i", i=4),
+                shares = (
+                    (nc.vector.tensor_copy, 0, VECTOR_EDGES[q]),
+                    (nc.scalar.copy, VECTOR_EDGES[q], QUARTER),
                 )
+                for copy, low, high in shares:
+                    if low < high:
+                        copy(
+                            out=grouped[:, PACK * low : PACK * high].rearrange("p (c i t) -> p c t i", i=4, t=PACK),
+                            in_=raw_rows[:, :, q * QUARTER + low : q * QUARTER + high].rearrange(
+                                "p t (c i) -> p c t i", i=4
+                            ),
+                        )
                 staged.append(grouped)
             e_mx = [quantize(staged[b], QUARTER, "e%d" % (2 * a + b)) for b in range(2)]
             for b in range(2):
                 q = 2 * a + b
                 e_codes, e_scales = e_mx[b]
+                for t in range(2, PACK):
+                    node_pass(weight, last, q, t)
                 for t in range(PACK):
                     nc.tensor.matmul_mx(
                         out=banks[q][:, t * QUARTER : (t + 1) * QUARTER],

@@ -21,7 +21,7 @@ K_PASS = P * PACK
 EDGES = V // 2
 QUARTER = EDGES // 2
 VECTOR_COLUMNS = 32
-VECTOR_EDGES = (88, 88, 64, 128)
+VECTOR_EDGES = (88, 88, 88, 128)
 
 
 def tile_picked_edgeup_gelu_p_kernel(
@@ -81,13 +81,7 @@ def tile_picked_edgeup_gelu_p_kernel(
             load_rows(rows, "w%d" % n)
             for n, rows in enumerate((w3, w1[0:K_PASS, :], w2[0:K_PASS, :], w1[K_PASS:K, :], w2[K_PASS:K, :]))
         ]
-        raw_e = keep.tile([P, PACK * V], F32)
-        e_flat = eT.rearrange("(p j) v -> p (j v)", j=PACK)
-        e_rows = eT.rearrange("(p j) v -> p j v", j=PACK)
-        raw_rows = raw_e[:].rearrange("p (j v) -> p j v", j=PACK)
-        nc.sync.dma_start(out=raw_e[:, 0 : V + EDGES], in_=e_flat[:, 0 : V + EDGES])
-        nc.sync.dma_start(out=raw_rows[:, 2:PACK, 0:EDGES], in_=e_rows[:, 2:PACK, 0:EDGES])
-        nc.sync.dma_start(out=raw_rows[:, 1:PACK, EDGES:V], in_=e_rows[:, 1:PACK, EDGES:V])
+        raw_e = [load_rows(eT[:, a * EDGES : (a + 1) * EDGES], "e%d" % a) for a in range(2)]
         w4w = keep.tile([P, 2 * N], U8, align_bytes=64)
         nc.sync.dma_start(out=w4w[:].bitcast(I32), in_=w4_words[0].bitcast(I32))
         for q in range(4):
@@ -173,7 +167,7 @@ def tile_picked_edgeup_gelu_p_kernel(
                     if low < high:
                         copy(
                             out=grouped[:, PACK * low : PACK * high].rearrange("p (c i t) -> p c t i", i=4, t=PACK),
-                            in_=raw_rows[:, :, q * QUARTER + low : q * QUARTER + high].rearrange(
+                            in_=raw_e[a][:, :, q % 2 * QUARTER + low : q % 2 * QUARTER + high].rearrange(
                                 "p t (c i) -> p c t i", i=4
                             ),
                         )

@@ -79,9 +79,12 @@ def tile_picked_edgeup_gelu_p_kernel(
         xw.append(load_words(1))
         raw_w = [
             load_rows(rows, "w%d" % n)
-            for n, rows in enumerate((w3, w1[0:K_PASS, :], w2[0:K_PASS, :], w1[K_PASS:K, :], w2[K_PASS:K, :]))
+            for n, rows in enumerate((w1[0:K_PASS, :], w2[0:K_PASS, :], w1[K_PASS:K, :], w2[K_PASS:K, :], w3))
         ]
-        raw_e = [load_rows(eT[:, a * EDGES : (a + 1) * EDGES], "e%d" % a) for a in range(2)]
+        first_half = load_rows(eT[:, 0:EDGES], "e01")
+        raw_e = [first_half[:, :, 0:QUARTER], first_half[:, :, QUARTER:EDGES]]
+        for q in range(2, 4):
+            raw_e.append(load_rows(eT[:, q * QUARTER : (q + 1) * QUARTER], "e%d" % q)[:])
         w4w = keep.tile([P, 2 * N], U8, align_bytes=64)
         nc.sync.dma_start(out=w4w[:].bitcast(I32), in_=w4_words[0].bitcast(I32))
         for q in range(4):
@@ -123,27 +126,22 @@ def tile_picked_edgeup_gelu_p_kernel(
                 nc.vector.quantize_mx(out=codes[:, cols].bitcast(FP8X4), scales=scales[:, cols], in_=parts[u][:])
             return codes, scales
 
-        def node_pass(weight, n, q, t):
-            z, side = divmod(n - 1, 2)
-            codes, scales = weight
-            cols = slice(side * V + q * QUARTER, side * V + (q + 1) * QUARTER)
-            nc.tensor.matmul_mx(
-                out=banks[q][:, t * QUARTER : (t + 1) * QUARTER],
-                lhsT=codes[:, t * P : (t + 1) * P].bitcast(FP8X4),
-                lhsT_scale=scales[:, t * P : (t + 1) * P],
-                rhs=picked[z][:, cols].bitcast(FP8X4),
-                rhs_scale=picked_scales[4 * z : P, cols],
-                start=n == 1 and t == 0,
-                stop=False,
-            )
-
-        w3_codes, w3_scales = weight_codes(0)
-        last = len(raw_w) - 1
-        for n in range(1, last + 1):
-            weight = weight_codes(n)
-            for t in range(PACK if n < last else 2):
+        for n in range(len(raw_w) - 1):
+            z, side = divmod(n, 2)
+            codes, scales = weight_codes(n)
+            for t in range(PACK):
                 for q in range(4):
-                    node_pass(weight, n, q, t)
+                    cols = slice(side * V + q * QUARTER, side * V + (q + 1) * QUARTER)
+                    nc.tensor.matmul_mx(
+                        out=banks[q][:, t * QUARTER : (t + 1) * QUARTER],
+                        lhsT=codes[:, t * P : (t + 1) * P].bitcast(FP8X4),
+                        lhsT_scale=scales[:, t * P : (t + 1) * P],
+                        rhs=picked[z][:, cols].bitcast(FP8X4),
+                        rhs_scale=picked_scales[4 * z : P, cols],
+                        start=n == 0 and t == 0,
+                        stop=False,
+                    )
+        w3_codes, w3_scales = weight_codes(len(raw_w) - 1)
 
         hidden = [
             keep.tile([P, PACK * width], BF16, name="hidden%d" % n, align_bytes=64)
@@ -167,7 +165,7 @@ def tile_picked_edgeup_gelu_p_kernel(
                     if low < high:
                         copy(
                             out=grouped[:, PACK * low : PACK * high].rearrange("p (c i t) -> p c t i", i=4, t=PACK),
-                            in_=raw_e[a][:, :, q % 2 * QUARTER + low : q % 2 * QUARTER + high].rearrange(
+                            in_=raw_e[q][:, :, low:high].rearrange(
                                 "p t (c i) -> p c t i", i=4
                             ),
                         )
@@ -176,8 +174,6 @@ def tile_picked_edgeup_gelu_p_kernel(
             for b in range(2):
                 q = 2 * a + b
                 e_codes, e_scales = e_mx[b]
-                for t in range(2, PACK):
-                    node_pass(weight, last, q, t)
                 for t in range(PACK):
                     nc.tensor.matmul_mx(
                         out=banks[q][:, t * QUARTER : (t + 1) * QUARTER],

@@ -63,6 +63,7 @@ def tile_picked_edgeup_gelu_p_kernel(
         nc.vector.memset(warm[:], 0.0)
         nc.scalar.activation(out=warm[:, 1:2], in_=warm[:, 0:1], func=GELU)
 
+        raw_w = [load_rows(w1[0:K_PASS, :], "w0")]
         xw = [load_words(0)]
         offsets = keep.tile([P, S // 16], U16)
         nc.sync.dma_start(offsets[:], offs)
@@ -76,11 +77,10 @@ def tile_picked_edgeup_gelu_p_kernel(
             nc.gpsimd.dma_start(
                 out=xs[32 * q : 32 * q + 8, :].bitcast(I32), in_=x_scales[:, 4 * q : 4 * q + 4, :].bitcast(I32)
             )
+        raw_w.append(load_rows(w2[0:K_PASS, :], "w1"))
         xw.append(load_words(1))
-        raw_w = [
-            load_rows(rows, "w%d" % n)
-            for n, rows in enumerate((w1[0:K_PASS, :], w2[0:K_PASS, :], w1[K_PASS:K, :], w2[K_PASS:K, :], w3))
-        ]
+        for rows in (w1[K_PASS:K, :], w2[K_PASS:K, :], w3):
+            raw_w.append(load_rows(rows, "w%d" % len(raw_w)))
         first_half = load_rows(eT[:, 0:EDGES], "e01")
         raw_e = [first_half[:, :, 0:QUARTER], first_half[:, :, QUARTER:EDGES]]
         for q in range(2, 4):
@@ -114,7 +114,7 @@ def tile_picked_edgeup_gelu_p_kernel(
                     in_=raw_w[n][:].rearrange("p j (m t) -> p m j t", t=PACK)[:, cols, :, 2 * u : 2 * u + 2],
                 )
 
-            cast(nc.scalar.copy if n < 2 else nc.vector.tensor_copy, 0, slice(0, P))
+            cast(nc.scalar.copy if n < 3 else nc.vector.tensor_copy, 0, slice(0, P))
             if n == len(raw_w) - 1:
                 cast(nc.vector.tensor_copy, 1, slice(0, VECTOR_COLUMNS))
                 cast(nc.scalar.copy, 1, slice(VECTOR_COLUMNS, P))

@@ -20,8 +20,6 @@ PACK = 4
 K_PASS = P * PACK
 EDGES = V // 2
 QUARTER = EDGES // 2
-VECTOR_COLUMNS = 32
-VECTOR_EDGES = (88, 88, 88, 128)
 
 
 def tile_picked_edgeup_gelu_p_kernel(
@@ -81,10 +79,7 @@ def tile_picked_edgeup_gelu_p_kernel(
         xw.append(load_words(1))
         for rows in (w1[K_PASS:K, :], w2[K_PASS:K, :], w3):
             raw_w.append(load_rows(rows, "w%d" % len(raw_w)))
-        first_half = load_rows(eT[:, 0:EDGES], "e01")
-        raw_e = [first_half[:, :, 0:QUARTER], first_half[:, :, QUARTER:EDGES]]
-        for q in range(2, 4):
-            raw_e.append(load_rows(eT[:, q * QUARTER : (q + 1) * QUARTER], "e%d" % q)[:])
+        raw_e = [load_rows(eT[:, q * QUARTER : (q + 1) * QUARTER], "e%d" % q) for q in range(4)]
         w4w = keep.tile([P, 2 * N], U8, align_bytes=64)
         nc.sync.dma_start(out=w4w[:].bitcast(I32), in_=w4_words[0].bitcast(I32))
         for q in range(4):
@@ -102,33 +97,30 @@ def tile_picked_edgeup_gelu_p_kernel(
         picked_scales = keep.tile([P, S], U8, align_bytes=64)
         nc.vector.tensor_copy(out=picked_scales[:], in_=xs[:].indirect(offsets[:]))
 
-        def weight_codes(n):
-            name = "w%d" % n
-            parts = [
-                keep.tile([P, PACK * 2 * P], BF16, name=name + "_bf16_%d" % u, align_bytes=64) for u in range(2)
-            ]
+        def cast_weight(n, u, copy):
+            part = keep.tile([P, PACK * 2 * P], BF16, name="w%d_bf16_%d" % (n, u), align_bytes=64)
+            copy(
+                out=part[:].rearrange("p (t m j) -> p m j t", t=2, j=PACK),
+                in_=raw_w[n][:].rearrange("p j (m t) -> p m j t", t=PACK)[:, :, :, 2 * u : 2 * u + 2],
+            )
+            return part
 
-            def cast(copy, u, cols):
-                copy(
-                    out=parts[u][:].rearrange("p (t m j) -> p m j t", t=2, j=PACK)[:, cols],
-                    in_=raw_w[n][:].rearrange("p j (m t) -> p m j t", t=PACK)[:, cols, :, 2 * u : 2 * u + 2],
-                )
+        def quantize_weight(mx, u, part):
+            cols = slice(2 * u * P, 2 * (u + 1) * P)
+            nc.vector.quantize_mx(out=mx[0][:, cols].bitcast(FP8X4), scales=mx[1][:, cols], in_=part[:])
 
-            cast(nc.scalar.copy if n < 3 else nc.vector.tensor_copy, 0, slice(0, P))
-            if n == len(raw_w) - 1:
-                cast(nc.vector.tensor_copy, 1, slice(0, VECTOR_COLUMNS))
-                cast(nc.scalar.copy, 1, slice(VECTOR_COLUMNS, P))
-            else:
-                cast(nc.scalar.copy, 1, slice(0, P))
-            codes, scales = mx_tiles(H, name, "xs" if n == 0 else None)
-            for u in range(2):
-                cols = slice(2 * u * P, 2 * (u + 1) * P)
-                nc.vector.quantize_mx(out=codes[:, cols].bitcast(FP8X4), scales=scales[:, cols], in_=parts[u][:])
-            return codes, scales
+        def cast_edges(q, grouped, copy, low, high):
+            copy(
+                out=grouped[:, PACK * low : PACK * high].rearrange("p (c i t) -> p c t i", i=4, t=PACK),
+                in_=raw_e[q][:, :, low:high].rearrange("p t (c i) -> p c t i", i=4),
+            )
 
         for n in range(len(raw_w) - 1):
             z, side = divmod(n, 2)
-            codes, scales = weight_codes(n)
+            parts = [cast_weight(n, 0, nc.scalar.copy if n < 3 else nc.vector.tensor_copy), cast_weight(n, 1, nc.scalar.copy)]
+            codes, scales = mx_tiles(H, "w%d" % n, "xs" if n == 0 else None)
+            for u in range(2):
+                quantize_weight((codes, scales), u, parts[u])
             for t in range(PACK):
                 for q in range(4):
                     cols = slice(side * V + q * QUARTER, side * V + (q + 1) * QUARTER)
@@ -141,7 +133,17 @@ def tile_picked_edgeup_gelu_p_kernel(
                         start=n == 0 and t == 0,
                         stop=False,
                     )
-        w3_codes, w3_scales = weight_codes(len(raw_w) - 1)
+
+        grouped = [keep.tile([P, PACK * QUARTER], BF16, name="e%d_bf16" % q, align_bytes=64) for q in range(4)]
+        e_mx = [mx_tiles(QUARTER, "e%d" % q) for q in range(4)]
+        w3_mx = mx_tiles(H, "w3q")
+
+        def quantize_edges(q, low, high):
+            nc.vector.quantize_mx(
+                out=e_mx[q][0][:, low:high].bitcast(FP8X4),
+                scales=e_mx[q][1][:, low:high],
+                in_=grouped[q][:, PACK * low : PACK * high],
+            )
 
         hidden = [
             keep.tile([P, PACK * width], BF16, name="hidden%d" % n, align_bytes=64)
@@ -153,42 +155,48 @@ def tile_picked_edgeup_gelu_p_kernel(
             hidden[1][:],
             hidden[2][:],
         )
-        for a in range(2):
-            staged = []
-            for q in (2 * a, 2 * a + 1):
-                grouped = keep.tile([P, PACK * QUARTER], BF16, name="e%d_bf16" % q, align_bytes=64)
-                shares = (
-                    (nc.vector.tensor_copy, 0, VECTOR_EDGES[q]),
-                    (nc.scalar.copy, VECTOR_EDGES[q], QUARTER),
+
+        def close_bank(q):
+            for t in range(PACK):
+                nc.tensor.matmul_mx(
+                    out=banks[q][:, t * QUARTER : (t + 1) * QUARTER],
+                    lhsT=w3_mx[0][:, t * P : (t + 1) * P].bitcast(FP8X4),
+                    lhsT_scale=w3_mx[1][:, t * P : (t + 1) * P],
+                    rhs=e_mx[q][0][:].bitcast(FP8X4),
+                    rhs_scale=e_mx[q][1][:],
+                    start=False,
+                    stop=t == PACK - 1,
                 )
-                for copy, low, high in shares:
-                    if low < high:
-                        copy(
-                            out=grouped[:, PACK * low : PACK * high].rearrange("p (c i t) -> p c t i", i=4, t=PACK),
-                            in_=raw_e[q][:, :, low:high].rearrange(
-                                "p t (c i) -> p c t i", i=4
-                            ),
-                        )
-                staged.append(grouped)
-            e_mx = [quantize(staged[b], QUARTER, "e%d" % (2 * a + b)) for b in range(2)]
-            for b in range(2):
-                q = 2 * a + b
-                e_codes, e_scales = e_mx[b]
-                for t in range(PACK):
-                    nc.tensor.matmul_mx(
-                        out=banks[q][:, t * QUARTER : (t + 1) * QUARTER],
-                        lhsT=w3_codes[:, t * P : (t + 1) * P].bitcast(FP8X4),
-                        lhsT_scale=w3_scales[:, t * P : (t + 1) * P],
-                        rhs=e_codes[:].bitcast(FP8X4),
-                        rhs_scale=e_scales[:],
-                        start=False,
-                        stop=t == PACK - 1,
-                    )
-                nc.scalar.activation(
-                    out=hidden_of[q].rearrange("p (v t) -> p v t", t=PACK),
-                    in_=banks[q][:].rearrange("p (t v) -> p v t", t=PACK),
-                    func=GELU,
-                )
+
+        def gelu(q):
+            nc.scalar.activation(
+                out=hidden_of[q].rearrange("p (v t) -> p v t", t=PACK),
+                in_=banks[q][:].rearrange("p (t v) -> p v t", t=PACK),
+                func=GELU,
+            )
+
+        last = len(raw_w) - 1
+        w3_parts = [cast_weight(last, 0, nc.vector.tensor_copy), cast_weight(last, 1, nc.scalar.copy)]
+        cast_edges(0, grouped[0], nc.vector.tensor_copy, 0, QUARTER)
+        quantize_weight(w3_mx, 0, w3_parts[0])
+        quantize_edges(0, 0, QUARTER)
+        quantize_weight(w3_mx, 1, w3_parts[1])
+        close_bank(0)
+        cast_edges(1, grouped[1], nc.scalar.copy, 0, QUARTER)
+        gelu(0)
+        cast_edges(2, grouped[2], nc.vector.tensor_copy, 0, QUARTER)
+        quantize_edges(1, 0, QUARTER)
+        close_bank(1)
+        gelu(1)
+        quantize_edges(2, 0, QUARTER)
+        close_bank(2)
+        gelu(2)
+        for half in range(2):
+            cast_edges(3, grouped[3], nc.vector.tensor_copy, 64 * half, 64 * (half + 1))
+        for half in range(2):
+            quantize_edges(3, 64 * half, 64 * (half + 1))
+        close_bank(3)
+        gelu(3)
 
         first = 0
         for n, width in enumerate((EDGES, QUARTER, QUARTER)):
@@ -204,7 +212,7 @@ def tile_picked_edgeup_gelu_p_kernel(
                 stop=True,
             )
             result = keep.tile([N, width], F32, name="result%d" % n)
-            copy = nc.scalar.copy if n == 2 else nc.vector.tensor_copy
+            copy = nc.scalar.copy if n > 0 else nc.vector.tensor_copy
             copy(out=result[:], in_=acc[:])
             nc.sync.dma_start(out=out[:, first : first + width], in_=result[:])
             first = first + width

@@ -145,16 +145,8 @@ def tile_picked_edgeup_gelu_p_kernel(
                 in_=grouped[q][:, PACK * low : PACK * high],
             )
 
-        hidden = [
-            keep.tile([P, PACK * width], BF16, name="hidden%d" % n, align_bytes=64)
-            for n, width in enumerate((EDGES, QUARTER, QUARTER))
-        ]
-        hidden_of = (
-            hidden[0][:, 0 : PACK * QUARTER],
-            hidden[0][:, PACK * QUARTER : PACK * EDGES],
-            hidden[1][:],
-            hidden[2][:],
-        )
+        hidden = keep.tile([P, PACK * V], BF16, name="hidden", align_bytes=64)
+        h_codes, h_scales = mx_tiles(V, "h")
 
         def close_bank(q):
             for t in range(PACK):
@@ -168,10 +160,11 @@ def tile_picked_edgeup_gelu_p_kernel(
                     stop=t == PACK - 1,
                 )
 
-        def gelu(q):
+        def gelu(q, low=0, high=QUARTER):
+            edges = slice(PACK * (q * QUARTER + low), PACK * (q * QUARTER + high))
             nc.scalar.activation(
-                out=hidden_of[q].rearrange("p (v t) -> p v t", t=PACK),
-                in_=banks[q][:].rearrange("p (t v) -> p v t", t=PACK),
+                out=hidden[:, edges].rearrange("p (v t) -> p v t", t=PACK),
+                in_=banks[q][:].rearrange("p (t v) -> p v t", t=PACK)[:, low:high],
                 func=GELU,
             )
 
@@ -196,23 +189,32 @@ def tile_picked_edgeup_gelu_p_kernel(
         for half in range(2):
             quantize_edges(3, 64 * half, 64 * (half + 1))
         close_bank(3)
-        gelu(3)
+        gelu(3, 0, 64)
+        gelu(3, 64, 128)
 
-        first = 0
-        for n, width in enumerate((EDGES, QUARTER, QUARTER)):
-            h_codes, h_scales = quantize(hidden[n], width, "h%d" % n)
-            acc = psum.tile([N, width], F32, name="acc%d" % n)
+
+        def second_product(low, high, copy, result):
+            nc.vector.quantize_mx(
+                out=h_codes[:, low:high].bitcast(FP8X4), scales=h_scales[:, low:high], in_=hidden[:, PACK * low : PACK * high]
+            )
+            start = min(low, high - QUARTER)
+            acc = psum.tile([N, high - start], F32, name="acc%d" % low)
             nc.tensor.matmul_mx(
                 out=acc[:],
                 lhsT=w4w[:].bitcast(FP4X4),
                 lhsT_scale=w4s[:],
-                rhs=h_codes[:].bitcast(FP8X4),
-                rhs_scale=h_scales[:],
+                rhs=h_codes[:, start:high].bitcast(FP8X4),
+                rhs_scale=h_scales[:, start:high],
                 start=True,
                 stop=True,
             )
-            result = keep.tile([N, width], F32, name="result%d" % n)
-            copy = nc.scalar.copy if n > 0 else nc.vector.tensor_copy
-            copy(out=result[:], in_=acc[:])
-            nc.sync.dma_start(out=out[:, first : first + width], in_=result[:])
-            first = first + width
+            copy(out=result, in_=acc[:, low - start :])
+
+        results = [keep.tile([N, width], F32, name="result%d" % n) for n, width in enumerate((EDGES, QUARTER, QUARTER))]
+        second_product(0, 256, nc.scalar.copy, results[0][:])
+        nc.sync.dma_start(out=out[:, 0:256], in_=results[0][:])
+        second_product(256, 384, nc.vector.tensor_copy, results[1][:])
+        nc.sync.dma_start(out=out[:, 256:384], in_=results[1][:])
+        second_product(384, 448, nc.vector.tensor_copy, results[2][:, 0:64])
+        second_product(448, 512, nc.scalar.copy, results[2][:, 64:128])
+        nc.sync.dma_start(out=out[:, 384:512], in_=results[2][:])

@@ -31,7 +31,7 @@ def tile_picked_edgeup_gelu_p_kernel(
         psum = ctx.enter_context(tc.psum_pool(name="psum", bufs=1))
 
         def load_rows(rows, name):
-            raw = keep.tile([P, PACK, rows.shape[1]], F32, name=name)
+            raw = keep.tile([P, PACK, rows.shape[1]], F32, name=name, align_bytes=64)
             nc.sync.dma_start(out=raw[:], in_=rows.rearrange("(p j) w -> p j w", j=PACK))
             return raw
 
@@ -97,13 +97,16 @@ def tile_picked_edgeup_gelu_p_kernel(
         picked_scales = keep.tile([P, S], U8, align_bytes=64)
         nc.vector.tensor_copy(out=picked_scales[:], in_=xs[:].indirect(offsets[:]))
 
-        def cast_weight(n, u, copy):
-            part = keep.tile([P, PACK * 2 * P], BF16, name="w%d_bf16_%d" % (n, u), align_bytes=64)
+        def stage_weight(n):
+            return [
+                keep.tile([P, PACK * 2 * P], BF16, name="w%d_bf16_%d" % (n, u), align_bytes=64) for u in range(2)
+            ]
+
+        def cast_weight(n, parts, u, copy, cols=slice(0, P)):
             copy(
-                out=part[:].rearrange("p (t m j) -> p m j t", t=2, j=PACK),
-                in_=raw_w[n][:].rearrange("p j (m t) -> p m j t", t=PACK)[:, :, :, 2 * u : 2 * u + 2],
+                out=parts[u][:].rearrange("p (t m j) -> p m j t", t=2, j=PACK)[:, cols],
+                in_=raw_w[n][:].rearrange("p j (m t) -> p m j t", t=PACK)[:, cols, :, 2 * u : 2 * u + 2],
             )
-            return part
 
         def quantize_weight(mx, u, part):
             cols = slice(2 * u * P, 2 * (u + 1) * P)
@@ -117,7 +120,9 @@ def tile_picked_edgeup_gelu_p_kernel(
 
         for n in range(len(raw_w) - 1):
             z, side = divmod(n, 2)
-            parts = [cast_weight(n, 0, nc.scalar.copy if n < 3 else nc.vector.tensor_copy), cast_weight(n, 1, nc.scalar.copy)]
+            parts = stage_weight(n)
+            cast_weight(n, parts, 0, nc.scalar.copy if n < 3 else nc.vector.tensor_copy)
+            cast_weight(n, parts, 1, nc.scalar.copy)
             codes, scales = mx_tiles(H, "w%d" % n, "xs" if n == 0 else None)
             for u in range(2):
                 quantize_weight((codes, scales), u, parts[u])
@@ -134,7 +139,10 @@ def tile_picked_edgeup_gelu_p_kernel(
                         stop=False,
                     )
 
-        grouped = [keep.tile([P, PACK * QUARTER], BF16, name="e%d_bf16" % q, align_bytes=64) for q in range(4)]
+        grouped = [
+            keep.tile([P, PACK * QUARTER], BF16, name="e%d_bf16" % q, tag=tag, align_bytes=64)
+            for q, tag in enumerate(("e0_bf16", "e1_bf16", "e1", "e2"))
+        ]
         e_mx = [mx_tiles(QUARTER, "e%d" % q) for q in range(4)]
         w3_mx = mx_tiles(H, "w3q")
 
@@ -169,7 +177,10 @@ def tile_picked_edgeup_gelu_p_kernel(
             )
 
         last = len(raw_w) - 1
-        w3_parts = [cast_weight(last, 0, nc.vector.tensor_copy), cast_weight(last, 1, nc.scalar.copy)]
+        w3_parts = stage_weight(last)
+        cast_weight(last, w3_parts, 0, nc.vector.tensor_copy)
+        cast_weight(last, w3_parts, 1, nc.vector.tensor_copy, slice(0, 32))
+        cast_weight(last, w3_parts, 1, nc.scalar.copy, slice(32, P))
         cast_edges(0, grouped[0], nc.vector.tensor_copy, 0, QUARTER)
         quantize_weight(w3_mx, 0, w3_parts[0])
         quantize_edges(0, 0, QUARTER)
@@ -177,18 +188,16 @@ def tile_picked_edgeup_gelu_p_kernel(
         close_bank(0)
         cast_edges(1, grouped[1], nc.scalar.copy, 0, QUARTER)
         gelu(0)
-        cast_edges(2, grouped[2], nc.vector.tensor_copy, 0, QUARTER)
         quantize_edges(1, 0, QUARTER)
         close_bank(1)
         gelu(1)
-        quantize_edges(2, 0, QUARTER)
-        close_bank(2)
+        for q in (2, 3):
+            for half in range(2):
+                cast_edges(q, grouped[q], nc.vector.tensor_copy, 64 * half, 64 * (half + 1))
+            for half in range(2):
+                quantize_edges(q, 64 * half, 64 * (half + 1))
+            close_bank(q)
         gelu(2)
-        for half in range(2):
-            cast_edges(3, grouped[3], nc.vector.tensor_copy, 64 * half, 64 * (half + 1))
-        for half in range(2):
-            quantize_edges(3, 64 * half, 64 * (half + 1))
-        close_bank(3)
         gelu(3, 0, 64)
         gelu(3, 64, 128)
 

@@ -187,16 +187,16 @@ def tile_picked_edgeup_gelu_p_kernel(
         quantize_weight(w3_mx, 1, w3_parts[1])
         close_bank(0)
         cast_edges(1, grouped[1], nc.scalar.copy, 0, QUARTER)
-        gelu(0)
         quantize_edges(1, 0, QUARTER)
         close_bank(1)
-        gelu(1)
-        for q in (2, 3):
-            for half in range(2):
-                cast_edges(q, grouped[q], nc.vector.tensor_copy, 64 * half, 64 * (half + 1))
+        for q, second in ((2, nc.scalar.copy), (3, nc.vector.tensor_copy)):
+            cast_edges(q, grouped[q], nc.vector.tensor_copy, 0, 64)
+            cast_edges(q, grouped[q], second, 64, QUARTER)
             for half in range(2):
                 quantize_edges(q, 64 * half, 64 * (half + 1))
             close_bank(q)
+        gelu(0)
+        gelu(1)
         gelu(2)
         gelu(3, 0, 64)
         gelu(3, 64, 128)

@@ -102,21 +102,24 @@ def tile_picked_edgeup_gelu_p_kernel(
                 keep.tile([P, PACK * 2 * P], BF16, name="w%d_bf16_%d" % (n, u), align_bytes=64) for u in range(2)
             ]
 
-        def cast_weight(n, parts, u, copy, cols=slice(0, P)):
+        def cast_weight(n, parts, u, copy):
             copy(
-                out=parts[u][:].rearrange("p (t m j) -> p m j t", t=2, j=PACK)[:, cols],
-                in_=raw_w[n][:].rearrange("p j (m t) -> p m j t", t=PACK)[:, cols, :, 2 * u : 2 * u + 2],
+                out=parts[u][:].rearrange("p (t m j) -> p m j t", t=2, j=PACK),
+                in_=raw_w[n][:].rearrange("p j (m t) -> p m j t", t=PACK)[:, :, :, 2 * u : 2 * u + 2],
             )
 
         def quantize_weight(mx, u, part):
             cols = slice(2 * u * P, 2 * (u + 1) * P)
             nc.vector.quantize_mx(out=mx[0][:, cols].bitcast(FP8X4), scales=mx[1][:, cols], in_=part[:])
 
-        def cast_edges(q, grouped, copy, low, high):
+        def cast_edges(q, low, high, copy, tag=None):
+            name = "e%d_%d_bf16" % (q, low)
+            staged = keep.tile([P, PACK * (high - low)], BF16, name=name, tag=tag or name, align_bytes=64)
             copy(
-                out=grouped[:, PACK * low : PACK * high].rearrange("p (c i t) -> p c t i", i=4, t=PACK),
+                out=staged[:].rearrange("p (c i t) -> p c t i", i=4, t=PACK),
                 in_=raw_e[q][:, :, low:high].rearrange("p t (c i) -> p c t i", i=4),
             )
+            return staged
 
         for n in range(len(raw_w) - 1):
             z, side = divmod(n, 2)
@@ -139,18 +142,12 @@ def tile_picked_edgeup_gelu_p_kernel(
                         stop=False,
                     )
 
-        grouped = [
-            keep.tile([P, PACK * QUARTER], BF16, name="e%d_bf16" % q, tag=tag, align_bytes=64)
-            for q, tag in enumerate(("e0_bf16", "e1_bf16", "e1", "e2"))
-        ]
         e_mx = [mx_tiles(QUARTER, "e%d" % q) for q in range(4)]
         w3_mx = mx_tiles(H, "w3q")
 
-        def quantize_edges(q, low, high):
+        def quantize_edges(q, low, high, staged):
             nc.vector.quantize_mx(
-                out=e_mx[q][0][:, low:high].bitcast(FP8X4),
-                scales=e_mx[q][1][:, low:high],
-                in_=grouped[q][:, PACK * low : PACK * high],
+                out=e_mx[q][0][:, low:high].bitcast(FP8X4), scales=e_mx[q][1][:, low:high], in_=staged[:]
             )
 
         hidden = keep.tile([P, PACK * V], BF16, name="hidden", align_bytes=64)
@@ -179,22 +176,23 @@ def tile_picked_edgeup_gelu_p_kernel(
         last = len(raw_w) - 1
         w3_parts = stage_weight(last)
         cast_weight(last, w3_parts, 0, nc.vector.tensor_copy)
-        cast_weight(last, w3_parts, 1, nc.vector.tensor_copy, slice(0, 32))
-        cast_weight(last, w3_parts, 1, nc.scalar.copy, slice(32, P))
-        cast_edges(0, grouped[0], nc.vector.tensor_copy, 0, QUARTER)
+        cast_weight(last, w3_parts, 1, nc.scalar.copy)
+        staged = cast_edges(0, 0, QUARTER, nc.vector.tensor_copy)
         quantize_weight(w3_mx, 0, w3_parts[0])
-        quantize_edges(0, 0, QUARTER)
+        quantize_edges(0, 0, QUARTER, staged)
         quantize_weight(w3_mx, 1, w3_parts[1])
         close_bank(0)
-        cast_edges(1, grouped[1], nc.scalar.copy, 0, QUARTER)
-        quantize_edges(1, 0, QUARTER)
-        close_bank(1)
-        for q, second in ((2, nc.scalar.copy), (3, nc.vector.tensor_copy)):
-            cast_edges(q, grouped[q], nc.vector.tensor_copy, 0, 64)
-            cast_edges(q, grouped[q], second, 64, QUARTER)
-            for half in range(2):
-                quantize_edges(q, 64 * half, 64 * (half + 1))
+        for q, tag in ((1, "w4"), (2, None)):
+            first = cast_edges(q, 0, 64, nc.scalar.copy)
+            second = cast_edges(q, 64, QUARTER, nc.vector.tensor_copy, tag)
+            quantize_edges(q, 0, 64, first)
+            quantize_edges(q, 64, QUARTER, second)
             close_bank(q)
+        first = cast_edges(3, 0, 64, nc.vector.tensor_copy, "e2")
+        second = cast_edges(3, 64, QUARTER, nc.vector.tensor_copy)
+        quantize_edges(3, 0, 64, first)
+        quantize_edges(3, 64, QUARTER, second)
+        close_bank(3)
         gelu(0)
         gelu(1)
         gelu(2)

@@ -124,9 +124,9 @@ def tile_picked_edgeup_gelu_p_kernel(
         for n in range(len(raw_w) - 1):
             z, side = divmod(n, 2)
             parts = stage_weight(n)
-            cast_weight(n, parts, 0, nc.scalar.copy if n < 3 else nc.vector.tensor_copy)
+            cast_weight(n, parts, 0, nc.scalar.copy if n in (1, 2) else nc.vector.tensor_copy)
             cast_weight(n, parts, 1, nc.scalar.copy)
-            codes, scales = mx_tiles(H, "w%d" % n, "xs" if n == 0 else None)
+            codes, scales = mx_tiles(H, "w%d" % n)
             for u in range(2):
                 quantize_weight((codes, scales), u, parts[u])
             for t in range(PACK):

@@ -151,7 +151,7 @@ def tile_picked_edgeup_gelu_p_kernel(
             )
 
         hidden = keep.tile([P, PACK * V], BF16, name="hidden", align_bytes=64)
-        h_codes, h_scales = mx_tiles(V, "h")
+        h_mx = [mx_tiles(QUARTER, "h%d" % q) for q in range(3)]
 
         def close_bank(q):
             for t in range(PACK):
@@ -173,6 +173,7 @@ def tile_picked_edgeup_gelu_p_kernel(
                 func=GELU,
             )
 
+        on_vector, on_scalar = nc.vector.tensor_copy, nc.scalar.copy
         last = len(raw_w) - 1
         w3_parts = stage_weight(last)
         cast_weight(last, w3_parts, 0, nc.vector.tensor_copy)
@@ -196,32 +197,41 @@ def tile_picked_edgeup_gelu_p_kernel(
         gelu(0)
         gelu(1)
         gelu(2)
-        gelu(3, 0, 64)
-        gelu(3, 64, 128)
+        gelu(3, 0, 96)
+        gelu(3, 96, 128)
 
 
-        def second_product(low, high, copy, result):
+        def quantize_hidden(mx, place, low, high):
+            cols = slice(place, place + high - low)
             nc.vector.quantize_mx(
-                out=h_codes[:, low:high].bitcast(FP8X4), scales=h_scales[:, low:high], in_=hidden[:, PACK * low : PACK * high]
+                out=mx[0][:, cols].bitcast(FP8X4), scales=mx[1][:, cols], in_=hidden[:, PACK * low : PACK * high]
             )
-            start = min(low, high - QUARTER)
-            acc = psum.tile([N, high - start], F32, name="acc%d" % low)
+
+        def second_product(mx, bank, copy, result):
+            acc = psum.tile([N, QUARTER], F32, name="acc_" + bank, tag=bank)
             nc.tensor.matmul_mx(
                 out=acc[:],
                 lhsT=w4w[:].bitcast(FP4X4),
                 lhsT_scale=w4s[:],
-                rhs=h_codes[:, start:high].bitcast(FP8X4),
-                rhs_scale=h_scales[:, start:high],
+                rhs=mx[0][:].bitcast(FP8X4),
+                rhs_scale=mx[1][:],
                 start=True,
                 stop=True,
             )
-            copy(out=result, in_=acc[:, low - start :])
+            copy(out=result, in_=acc[:, 0 : result.shape[1]])
 
         results = [keep.tile([N, width], F32, name="result%d" % n) for n, width in enumerate((EDGES, QUARTER, QUARTER))]
-        second_product(0, 256, nc.scalar.copy, results[0][:])
+        quantize_hidden(h_mx[0], 0, 0, 128)
+        second_product(h_mx[0], "h0", on_vector, results[0][:, 0:128])
+        quantize_hidden(h_mx[1], 0, 128, 256)
+        second_product(h_mx[1], "acc1", on_scalar, results[0][:, 128:256])
         nc.sync.dma_start(out=out[:, 0:256], in_=results[0][:])
-        second_product(256, 384, nc.vector.tensor_copy, results[1][:])
+        quantize_hidden(h_mx[2], 0, 256, 384)
+        quantize_hidden(h_mx[0], 0, 384, 448)
+        quantize_hidden(h_mx[0], 64, 448, 480)
+        quantize_hidden(h_mx[1], 0, 480, 512)
+        second_product(h_mx[2], "acc2", on_vector, results[1][:])
         nc.sync.dma_start(out=out[:, 256:384], in_=results[1][:])
-        second_product(384, 448, nc.vector.tensor_copy, results[2][:, 0:64])
-        second_product(448, 512, nc.scalar.copy, results[2][:, 64:128])
+        second_product(h_mx[0], "acc3", on_vector, results[2][:, 0:96])
+        second_product(h_mx[1], "acc4", on_scalar, results[2][:, 96:128])
         nc.sync.dma_start(out=out[:, 384:512], in_=results[2][:])

@@ -54,11 +54,9 @@ def tile_picked_edgeup_gelu_p_kernel(
 
         xs = keep.tile([P, T], U8, tag="xs", align_bytes=64)
         w4s = keep.tile([P, N], U8, align_bytes=64)
-        nc.gpsimd.memset(xs[:].bitcast(I32), 0)
-        nc.vector.memset(w4s[:].bitcast(I32), 0)
-
         warm = keep.tile([P, 2], F32)
-        nc.vector.memset(warm[:], 0.0)
+        nc.gpsimd.memset(warm[:], 0.0)
+        nc.gpsimd.memset(xs[:].bitcast(I32), 0)
         nc.scalar.activation(out=warm[:, 1:2], in_=warm[:, 0:1], func=GELU)
 
         raw_w = [load_rows(w1[0:K_PASS, :], "w0")]
@@ -75,6 +73,7 @@ def tile_picked_edgeup_gelu_p_kernel(
             nc.gpsimd.dma_start(
                 out=xs[32 * q : 32 * q + 8, :].bitcast(I32), in_=x_scales[:, 4 * q : 4 * q + 4, :].bitcast(I32)
             )
+        nc.gpsimd.memset(w4s[:].bitcast(I32), 0)
         raw_w.append(load_rows(w2[0:K_PASS, :], "w1"))
         xw.append(load_words(1))
         for rows in (w1[K_PASS:K, :], w2[K_PASS:K, :], w3):
@@ -98,27 +97,35 @@ def tile_picked_edgeup_gelu_p_kernel(
         nc.vector.tensor_copy(out=picked_scales[:], in_=xs[:].indirect(offsets[:]))
 
         def stage_weight(n):
+            if n < 2:
+                staged = keep.tile([P, PACK * H], BF16, name="w%d_bf16" % n, align_bytes=64)
+                return [staged[:, 0 : 2 * H], staged[:, 2 * H : 4 * H], staged[:]]
             return [
-                keep.tile([P, PACK * 2 * P], BF16, name="w%d_bf16_%d" % (n, u), align_bytes=64) for u in range(2)
+                keep.tile([P, 2 * H], BF16, name="w%d_bf16_%d" % (n, u), align_bytes=64)[:] for u in range(2)
             ]
 
         def cast_weight(n, parts, u, copy):
             copy(
-                out=parts[u][:].rearrange("p (t m j) -> p m j t", t=2, j=PACK),
+                out=parts[u].rearrange("p (t m j) -> p m j t", t=2, j=PACK),
                 in_=raw_w[n][:].rearrange("p j (m t) -> p m j t", t=PACK)[:, :, :, 2 * u : 2 * u + 2],
             )
 
         def quantize_weight(mx, u, part):
             cols = slice(2 * u * P, 2 * (u + 1) * P)
-            nc.vector.quantize_mx(out=mx[0][:, cols].bitcast(FP8X4), scales=mx[1][:, cols], in_=part[:])
+            nc.vector.quantize_mx(out=mx[0][:, cols].bitcast(FP8X4), scales=mx[1][:, cols], in_=part)
 
-        def cast_edges(q, low, high, copy, tag=None):
+        def cast_edges(q, low, high, shares, tag=None):
             name = "e%d_%d_bf16" % (q, low)
             staged = keep.tile([P, PACK * (high - low)], BF16, name=name, tag=tag or name, align_bytes=64)
-            copy(
-                out=staged[:].rearrange("p (c i t) -> p c t i", i=4, t=PACK),
-                in_=raw_e[q][:, :, low:high].rearrange("p t (c i) -> p c t i", i=4),
-            )
+            start = low
+            for copy, count in shares:
+                copy(
+                    out=staged[:, PACK * (start - low) : PACK * (start - low + count)].rearrange(
+                        "p (c i t) -> p c t i", i=4, t=PACK
+                    ),
+                    in_=raw_e[q][:, :, start : start + count].rearrange("p t (c i) -> p c t i", i=4),
+                )
+                start += count
             return staged
 
         for n in range(len(raw_w) - 1):
@@ -127,8 +134,11 @@ def tile_picked_edgeup_gelu_p_kernel(
             cast_weight(n, parts, 0, nc.scalar.copy if n in (1, 2) else nc.vector.tensor_copy)
             cast_weight(n, parts, 1, nc.scalar.copy)
             codes, scales = mx_tiles(H, "w%d" % n)
-            for u in range(2):
-                quantize_weight((codes, scales), u, parts[u])
+            if n < 2:
+                nc.vector.quantize_mx(out=codes[:].bitcast(FP8X4), scales=scales[:], in_=parts[2])
+            else:
+                for u in range(2):
+                    quantize_weight((codes, scales), u, parts[u])
             for t in range(PACK):
                 for q in range(4):
                     cols = slice(side * V + q * QUARTER, side * V + (q + 1) * QUARTER)
@@ -178,22 +188,20 @@ def tile_picked_edgeup_gelu_p_kernel(
         w3_parts = stage_weight(last)
         cast_weight(last, w3_parts, 0, nc.vector.tensor_copy)
         cast_weight(last, w3_parts, 1, nc.scalar.copy)
-        staged = cast_edges(0, 0, QUARTER, nc.vector.tensor_copy)
+        staged = cast_edges(0, 0, QUARTER, [(on_vector, QUARTER)])
         quantize_weight(w3_mx, 0, w3_parts[0])
         quantize_edges(0, 0, QUARTER, staged)
         quantize_weight(w3_mx, 1, w3_parts[1])
         close_bank(0)
-        for q, tag in ((1, "w4"), (2, None)):
-            first = cast_edges(q, 0, 64, nc.scalar.copy)
-            second = cast_edges(q, 64, QUARTER, nc.vector.tensor_copy, tag)
+        staged = cast_edges(1, 0, QUARTER, [(on_scalar, 96), (on_vector, 32)], "w4")
+        quantize_edges(1, 0, QUARTER, staged)
+        close_bank(1)
+        for q, engine, tag in ((2, on_scalar, None), (3, on_vector, "e2")):
+            first = cast_edges(q, 0, 64, [(engine, 64)], tag)
+            second = cast_edges(q, 64, QUARTER, [(on_vector, 64)])
             quantize_edges(q, 0, 64, first)
             quantize_edges(q, 64, QUARTER, second)
             close_bank(q)
-        first = cast_edges(3, 0, 64, nc.vector.tensor_copy, "e2")
-        second = cast_edges(3, 64, QUARTER, nc.vector.tensor_copy)
-        quantize_edges(3, 0, 64, first)
-        quantize_edges(3, 64, QUARTER, second)
-        close_bank(3)
         gelu(0)
         gelu(1)
         gelu(2)

@@ -131,9 +131,9 @@ def tile_picked_edgeup_gelu_p_kernel(
         for n in range(len(raw_w) - 1):
             z, side = divmod(n, 2)
             parts = stage_weight(n)
-            cast_weight(n, parts, 0, nc.scalar.copy if n in (1, 2) else nc.vector.tensor_copy)
+            cast_weight(n, parts, 0, nc.scalar.copy if n < 3 else nc.vector.tensor_copy)
             cast_weight(n, parts, 1, nc.scalar.copy)
-            codes, scales = mx_tiles(H, "w%d" % n)
+            codes, scales = mx_tiles(H, "w%d" % n, "xs" if n == 0 else None)
             if n < 2:
                 nc.vector.quantize_mx(out=codes[:].bitcast(FP8X4), scales=scales[:], in_=parts[2])
             else:
@@ -191,14 +191,22 @@ def tile_picked_edgeup_gelu_p_kernel(
         staged = cast_edges(0, 0, QUARTER, [(on_vector, QUARTER)])
         quantize_weight(w3_mx, 0, w3_parts[0])
         quantize_edges(0, 0, QUARTER, staged)
-        quantize_weight(w3_mx, 1, w3_parts[1])
+        for t in range(2, PACK):
+            cols = slice(t * P, (t + 1) * P)
+            nc.vector.quantize_mx(
+                out=w3_mx[0][:, cols].bitcast(FP8X4),
+                scales=w3_mx[1][:, cols],
+                in_=w3_parts[1][:, (t - 2) * K_PASS : (t - 1) * K_PASS],
+            )
         close_bank(0)
-        staged = cast_edges(1, 0, QUARTER, [(on_scalar, 96), (on_vector, 32)], "w4")
-        quantize_edges(1, 0, QUARTER, staged)
-        close_bank(1)
-        for q, engine, tag in ((2, on_scalar, None), (3, on_vector, "e2")):
-            first = cast_edges(q, 0, 64, [(engine, 64)], tag)
-            second = cast_edges(q, 64, QUARTER, [(on_vector, 64)])
+        plans = (
+            (1, [(on_scalar, 64)], [(on_scalar, 64)], None, None),
+            (2, [(on_scalar, 64)], [(on_vector, 64)], None, None),
+            (3, [(on_vector, 64)], [(on_vector, 64)], "e2", None),
+        )
+        for q, first_shares, second_shares, first_tag, second_tag in plans:
+            first = cast_edges(q, 0, 64, first_shares, first_tag)
+            second = cast_edges(q, 64, QUARTER, second_shares, second_tag)
             quantize_edges(q, 0, 64, first)
             quantize_edges(q, 64, QUARTER, second)
             close_bank(q)
@@ -238,7 +246,7 @@ def tile_picked_edgeup_gelu_p_kernel(
         quantize_hidden(h_mx[0], 0, 384, 448)
         quantize_hidden(h_mx[0], 64, 448, 480)
         quantize_hidden(h_mx[1], 0, 480, 512)
-        second_product(h_mx[2], "acc2", on_vector, results[1][:])
+        second_product(h_mx[2], "acc2", on_scalar, results[1][:])
         nc.sync.dma_start(out=out[:, 256:384], in_=results[1][:])
         second_product(h_mx[0], "acc3", on_vector, results[2][:, 0:96])
         second_product(h_mx[1], "acc4", on_scalar, results[2][:, 96:128])

from contextlib import ExitStack

import concourse.mybir as mybir

K, T, S, V, H, N, J = 1024, 2048, 1024, 512, 512, 128, 512
FLOPS = 2 * (2 * K * H * V + J * H * V + H * N * V)

F32 = mybir.dt.float32
BF16 = mybir.dt.bfloat16
I32 = mybir.dt.int32
U32 = mybir.dt.uint32
U16 = mybir.dt.uint16
U8 = mybir.dt.uint8
FP8X4 = mybir.dt.float8_e4m3fn_x4
FP4X4 = mybir.dt.float4_e2m1fn_x4
GELU = mybir.ActivationFunctionType.Gelu_apprx_tanh

P = 128
PACK = 4
K_PASS = P * PACK
EDGES = V // 2
QUARTER = EDGES // 2


def tile_picked_edgeup_gelu_p_kernel(
    tc, x_words, x_scales, eT, w1, w2, w3, w4_words, w4_scales, offs, out
):
    nc = tc.nc
    with ExitStack() as ctx:
        keep = ctx.enter_context(tc.tile_pool(name="keep", bufs=1))
        psum = ctx.enter_context(tc.psum_pool(name="psum", bufs=1))

        def load_rows(rows, name):
            raw = keep.tile([P, PACK, rows.shape[1]], F32, name=name, align_bytes=64)
            nc.sync.dma_start(out=raw[:], in_=rows.rearrange("(p j) w -> p j w", j=PACK))
            return raw

        def mx_tiles(width, name, scale_tag=None):
            codes = keep.tile([P, width], U32, name=name + "_codes", align_bytes=64)
            scales = keep.tile([P, width], U8, name=name + "_scales", tag=scale_tag or name + "_scales", align_bytes=64)
            return codes, scales

        def quantize(grouped, width, name):
            codes, scales = mx_tiles(width, name)
            nc.vector.quantize_mx(out=codes[:].bitcast(FP8X4), scales=scales[:], in_=grouped[:])
            return codes, scales

        def load_words(z):
            words = keep.tile([P, T], U32, name="x_words%d" % z, align_bytes=64)
            nc.sync.dma_start(
                out=words[:].bitcast(I32), in_=x_words[z].rearrange("p n t -> p (n t)").bitcast(I32)
            )
            return words

        xs = keep.tile([P, T], U8, tag="xs", align_bytes=64)
        w4s = keep.tile([P, N], U8, align_bytes=64)
        warm = keep.tile([P, 2], F32)
        nc.gpsimd.memset(warm[:], 0.0)
        nc.gpsimd.memset(xs[:].bitcast(I32), 0)
        nc.scalar.activation(out=warm[:, 1:2], in_=warm[:, 0:1], func=GELU)

        raw_w = [load_rows(w1[0:K_PASS, :], "w0")]
        xw = [load_words(0)]
        offsets = keep.tile([P, S // 16], U16)
        nc.sync.dma_start(offsets[:], offs)
        for q in range(2):
            for z in range(2):
                nc.sync.dma_start(
                    out=xs[32 * q + 4 * z : 32 * q + 4 * z + 4, :].bitcast(I32),
                    in_=x_scales[z, 4 * q : 4 * q + 4, :].bitcast(I32),
                )
        for q in range(2, 4):
            nc.gpsimd.dma_start(
                out=xs[32 * q : 32 * q + 8, :].bitcast(I32), in_=x_scales[:, 4 * q : 4 * q + 4, :].bitcast(I32)
            )
        nc.gpsimd.memset(w4s[:].bitcast(I32), 0)
        raw_w.append(load_rows(w2[0:K_PASS, :], "w1"))
        xw.append(load_words(1))
        for rows in (w1[K_PASS:K, :], w2[K_PASS:K, :], w3):
            raw_w.append(load_rows(rows, "w%d" % len(raw_w)))
        raw_e = [load_rows(eT[:, q * QUARTER : (q + 1) * QUARTER], "e%d" % q) for q in range(4)]
        w4w = keep.tile([P, 2 * N], U8, align_bytes=64)
        nc.sync.dma_start(out=w4w[:].bitcast(I32), in_=w4_words[0].bitcast(I32))
        for q in range(4):
            nc.sync.dma_start(
                out=w4s[32 * q : 32 * q + 4, :].bitcast(I32), in_=w4_scales[0, 4 * q : 4 * q + 4, :].bitcast(I32)
            )

        banks = [psum.tile([P, PACK * QUARTER], F32, name="h%d" % q) for q in range(4)]

        picked = []
        for z in range(2):
            words = keep.tile([P, S], U32, name="picked%d" % z, align_bytes=64)
            nc.vector.tensor_copy(out=words[:], in_=xw[z][:].indirect(offsets[:]))
            picked.append(words)
        picked_scales = keep.tile([P, S], U8, align_bytes=64)
        nc.vector.tensor_copy(out=picked_scales[:], in_=xs[:].indirect(offsets[:]))

        def stage_weight(n):
            if n < 2:
                staged = keep.tile([P, PACK * H], BF16, name="w%d_bf16" % n, align_bytes=64)
                return [staged[:, 0 : 2 * H], staged[:, 2 * H : 4 * H], staged[:]]
            return [
                keep.tile([P, 2 * H], BF16, name="w%d_bf16_%d" % (n, u), align_bytes=64)[:] for u in range(2)
            ]

        def cast_weight(n, parts, u, copy):
            copy(
                out=parts[u].rearrange("p (t m j) -> p m j t", t=2, j=PACK),
                in_=raw_w[n][:].rearrange("p j (m t) -> p m j t", t=PACK)[:, :, :, 2 * u : 2 * u + 2],
            )

        def quantize_weight(mx, u, part):
            cols = slice(2 * u * P, 2 * (u + 1) * P)
            nc.vector.quantize_mx(out=mx[0][:, cols].bitcast(FP8X4), scales=mx[1][:, cols], in_=part)

        def cast_edges(q, low, high, shares, tag=None):
            name = "e%d_%d_bf16" % (q, low)
            staged = keep.tile([P, PACK * (high - low)], BF16, name=name, tag=tag or name, align_bytes=64)
            start = low
            for copy, count in shares:
                copy(
                    out=staged[:, PACK * (start - low) : PACK * (start - low + count)].rearrange(
                        "p (c i t) -> p c t i", i=4, t=PACK
                    ),
                    in_=raw_e[q][:, :, start : start + count].rearrange("p t (c i) -> p c t i", i=4),
                )
                start += count
            return staged

        for n in range(len(raw_w) - 1):
            z, side = divmod(n, 2)
            parts = stage_weight(n)
            cast_weight(n, parts, 0, nc.scalar.copy if n < 3 else nc.vector.tensor_copy)
            cast_weight(n, parts, 1, nc.scalar.copy)
            codes, scales = mx_tiles(H, "w%d" % n, "xs" if n == 0 else None)
            if n < 2:
                nc.vector.quantize_mx(out=codes[:].bitcast(FP8X4), scales=scales[:], in_=parts[2])
            else:
                for u in range(2):
                    quantize_weight((codes, scales), u, parts[u])
            for t in range(PACK):
                for q in range(4):
                    cols = slice(side * V + q * QUARTER, side * V + (q + 1) * QUARTER)
                    nc.tensor.matmul_mx(
                        out=banks[q][:, t * QUARTER : (t + 1) * QUARTER],
                        lhsT=codes[:, t * P : (t + 1) * P].bitcast(FP8X4),
                        lhsT_scale=scales[:, t * P : (t + 1) * P],
                        rhs=picked[z][:, cols].bitcast(FP8X4),
                        rhs_scale=picked_scales[4 * z : P, cols],
                        start=n == 0 and t == 0,
                        stop=False,
                    )

        e_mx = [mx_tiles(QUARTER, "e%d" % q) for q in range(4)]
        w3_mx = mx_tiles(H, "w3q")

        def quantize_edges(q, low, high, staged):
            nc.vector.quantize_mx(
                out=e_mx[q][0][:, low:high].bitcast(FP8X4), scales=e_mx[q][1][:, low:high], in_=staged[:]
            )

        hidden = keep.tile([P, PACK * V], BF16, name="hidden", align_bytes=64)
        h_mx = [mx_tiles(QUARTER, "h%d" % q) for q in range(3)]

        def close_bank(q):
            for t in range(PACK):
                nc.tensor.matmul_mx(
                    out=banks[q][:, t * QUARTER : (t + 1) * QUARTER],
                    lhsT=w3_mx[0][:, t * P : (t + 1) * P].bitcast(FP8X4),
                    lhsT_scale=w3_mx[1][:, t * P : (t + 1) * P],
                    rhs=e_mx[q][0][:].bitcast(FP8X4),
                    rhs_scale=e_mx[q][1][:],
                    start=False,
                    stop=t == PACK - 1,
                )

        def gelu(q, low=0, high=QUARTER):
            edges = slice(PACK * (q * QUARTER + low), PACK * (q * QUARTER + high))
            nc.scalar.activation(
                out=hidden[:, edges].rearrange("p (v t) -> p v t", t=PACK),
                in_=banks[q][:].rearrange("p (t v) -> p v t", t=PACK)[:, low:high],
                func=GELU,
            )

        on_vector, on_scalar = nc.vector.tensor_copy, nc.scalar.copy
        last = len(raw_w) - 1
        w3_parts = stage_weight(last)
        cast_weight(last, w3_parts, 0, nc.vector.tensor_copy)
        cast_weight(last, w3_parts, 1, nc.scalar.copy)
        staged = cast_edges(0, 0, QUARTER, [(on_vector, QUARTER)])
        quantize_weight(w3_mx, 0, w3_parts[0])
        quantize_edges(0, 0, QUARTER, staged)
        for t in range(2, PACK):
            cols = slice(t * P, (t + 1) * P)
            nc.vector.quantize_mx(
                out=w3_mx[0][:, cols].bitcast(FP8X4),
                scales=w3_mx[1][:, cols],
                in_=w3_parts[1][:, (t - 2) * K_PASS : (t - 1) * K_PASS],
            )
        close_bank(0)
        plans = (
            (1, [(on_scalar, 64)], [(on_scalar, 64)], None, None),
            (2, [(on_scalar, 64)], [(on_vector, 64)], None, None),
            (3, [(on_vector, 64)], [(on_vector, 64)], "e2", None),
        )
        for q, first_shares, second_shares, first_tag, second_tag in plans:
            first = cast_edges(q, 0, 64, first_shares, first_tag)
            second = cast_edges(q, 64, QUARTER, second_shares, second_tag)
            quantize_edges(q, 0, 64, first)
            quantize_edges(q, 64, QUARTER, second)
            close_bank(q)
        gelu(0)
        gelu(1)
        gelu(2)
        gelu(3, 0, 96)
        gelu(3, 96, 128)


        def quantize_hidden(mx, place, low, high):
            cols = slice(place, place + high - low)
            nc.vector.quantize_mx(
                out=mx[0][:, cols].bitcast(FP8X4), scales=mx[1][:, cols], in_=hidden[:, PACK * low : PACK * high]
            )

        def second_product(mx, bank, copy, result):
            acc = psum.tile([N, QUARTER], F32, name="acc_" + bank, tag=bank)
            nc.tensor.matmul_mx(
                out=acc[:],
                lhsT=w4w[:].bitcast(FP4X4),
                lhsT_scale=w4s[:],
                rhs=mx[0][:].bitcast(FP8X4),
                rhs_scale=mx[1][:],
                start=True,
                stop=True,
            )
            copy(out=result, in_=acc[:, 0 : result.shape[1]])

        results = [keep.tile([N, width], F32, name="result%d" % n) for n, width in enumerate((EDGES, QUARTER, QUARTER))]
        quantize_hidden(h_mx[0], 0, 0, 128)
        second_product(h_mx[0], "h0", on_vector, results[0][:, 0:128])
        quantize_hidden(h_mx[1], 0, 128, 256)
        second_product(h_mx[1], "acc1", on_scalar, results[0][:, 128:256])
        nc.sync.dma_start(out=out[:, 0:256], in_=results[0][:])
        quantize_hidden(h_mx[2], 0, 256, 384)
        quantize_hidden(h_mx[0], 0, 384, 448)
        quantize_hidden(h_mx[0], 64, 448, 480)
        quantize_hidden(h_mx[1], 0, 480, 512)
        second_product(h_mx[2], "acc2", on_scalar, results[1][:])
        nc.sync.dma_start(out=out[:, 256:384], in_=results[1][:])
        second_product(h_mx[0], "acc3", on_vector, results[2][:, 0:96])
        second_product(h_mx[1], "acc4", on_scalar, results[2][:, 96:128])
        nc.sync.dma_start(out=out[:, 384:512], in_=results[2][:])
